import numpy as np
import ml_dtypes


def mxq(x, axis, fmt="e4m3"):
    dtype, down = {"e4m3": (ml_dtypes.float8_e4m3fn, 7), "e5m2": (ml_dtypes.float8_e5m2, 14)}[fmt]
    v = np.moveaxis(np.asarray(x, np.float32).astype(ml_dtypes.bfloat16).astype(np.float64), axis, -1)
    blocks = v.reshape(v.shape[:-1] + (-1, 32))
    amax = np.abs(blocks).max(-1, keepdims=True)
    byte = np.maximum(np.where(amax > 0, np.frexp(amax)[1] - 1 + 127, 0) - down, 1)
    scale = np.exp2(byte - 127.0)
    codes = (blocks / scale).astype(np.float32).astype(dtype).astype(np.float64)
    return np.moveaxis((codes * scale).reshape(v.shape), -1, axis)


WIDE = False


def mx_kscale(k):
    if not WIDE:
        return np.ones(k)
    levels = np.array([10, -10, 5, -5, 0])
    if k % 512:
        return np.exp2(np.random.permutation(np.resize(levels, k // 32))).repeat(32)
    a = np.empty((k // 512, 16))
    for p in range(k // 512):
        a[p, :8] = np.random.permutation(np.resize(levels, 8))
        for g in range(8):
            far = levels[np.abs(levels - a[p, g]) >= 10]
            a[p, g + 8] = far[np.random.randint(len(far))]
    return np.exp2(a.ravel()).repeat(32)


def f64(x):
    return np.asarray(x).astype(np.float64)


def striped(idx):
    return np.tile(idx.reshape(-1, 16).T, (8, 1)).astype(np.uint16)


def unstriped(offs):
    return offs[:16].T.reshape(-1).astype(np.int64)


def striped8(idx):
    return np.concatenate([x.reshape(-1, 16).T for x in idx]).astype(np.uint16)


def runs(offs, k):
    lists = np.stack([offs[16 * r : 16 * r + 16].T.reshape(-1) for r in range(8)]).astype(np.int64)
    return lists[np.arange(k) % 512 // 64]


def pack_weight(w):
    k, n = w.shape
    w = f64(np.asarray(w, np.float32).astype(ml_dtypes.bfloat16)).reshape(k // 32, 32, n)
    amax = np.abs(w).max(1)
    byte = np.clip(np.where(amax > 0, np.frexp(amax)[1] - 1 + 127 - 7, 1), 1, 254)
    scaled = (w * np.exp2(127.0 - byte)[:, None, :]).reshape(k, n).astype(np.float32)
    words = np.ascontiguousarray(scaled.reshape(k // 512, 128, 4, n).transpose(0, 1, 3, 2)).astype(ml_dtypes.float8_e4m3fn).view(np.uint8)
    return words, np.ascontiguousarray(byte.astype(np.uint8).reshape(k // 512, 16, n))


def unpack_weight(words, scales):
    g, p, n, _ = words.shape
    vals = np.ascontiguousarray(words).view(ml_dtypes.float8_e4m3fn).astype(np.float64) * np.repeat(np.exp2(scales.astype(np.float64) - 127.0), 8, axis=1)[..., None]
    return vals.transpose(0, 1, 3, 2).reshape(g * 512, n)


def relu(v):
    return np.maximum(v, 0.0)

def planes(y):
    n, m = y.shape
    v = y.astype(np.float32).astype(ml_dtypes.bfloat16).astype(np.float64).reshape(n // 32, 32, m)
    top = np.abs(v).max(1)
    byte = np.clip(np.where(top > 0, np.frexp(top)[1] - 1 + 127 - 7, 1), 1, 254)
    codes = (v * np.exp2(127.0 - byte)[:, None, :]).reshape(n, m).astype(np.float32).astype(ml_dtypes.float8_e4m3fn).view(np.uint8)
    words = codes.reshape(n // 512, 128, 4, m).transpose(0, 1, 3, 2)
    return np.ascontiguousarray(words), np.ascontiguousarray(byte.astype(np.uint8).reshape(n // 512, 16, m))


K, T, S, N, H = 512, 2048, 512, 512, 512


def setup_inputs():
    n = np.random.standard_normal
    s = mx_kscale(K)[:, None]
    u = mx_kscale(H)
    packed_xT = pack_weight(n((K, T)) * s)
    packed_w2 = pack_weight(n((H, N)) / np.sqrt(H) / u[:, None])
    return {
        "x_words": packed_xT[0],
        "x_scales": packed_xT[1],
        "w1": (n((K, H)) / np.sqrt(K) / s * u).astype(np.float32),
        "w2_words": packed_w2[0],
        "w2_scales": packed_w2[1],
        "offs": striped(np.random.permutation(T)[:S]),
        "par": striped8(np.random.randint(0, S, (8, S))),
    }


def reference(x_words, x_scales, w1, w2_words, w2_scales, offs, par):
    xq = unpack_weight(x_words, x_scales)[:, unstriped(offs)]
    y = mxq(f64(w1), 0, "e4m3").T @ xq
    p = y[np.arange(H)[:, None], runs(par, H)]
    q = p[np.arange(H)[:, None], runs(par, H)]
    z = relu(y + p - q)
    out_0 = unpack_weight(w2_words, w2_scales).T @ mxq(z, 0, "e4m3")
    return (out_0,) + planes(out_0)

@@ -1,0 +1,208 @@
+from contextlib import ExitStack
+
+import concourse.mybir as mybir
+
+K, T, S, H, N = 512, 2048, 512, 512, 512
+FLOPS = 2 * K * H * S + 2 * H * N * S
+
+F32 = mybir.dt.float32
+BF16 = mybir.dt.bfloat16
+I32 = mybir.dt.int32
+U32 = mybir.dt.uint32
+U16 = mybir.dt.uint16
+U8 = mybir.dt.uint8
+FP8X4 = mybir.dt.float8_e4m3fn_x4
+ALU = mybir.AluOpType
+ACT = mybir.ActivationFunctionType
+
+P = 128
+PACK = 4
+HALF = S // 2
+PIECE = 128
+W1_SPLIT = 80
+
+
+def tile_picked_ptrjump_relu_po_kernel(
+    tc, x_words, x_scales, w1, w2_words, w2_scales, offs, par, out_0, out_1, out_2
+):
+    nc = tc.nc
+    with ExitStack() as ctx:
+        lists = ctx.enter_context(tc.tile_pool(name="lists", bufs=1))
+        keep = ctx.enter_context(tc.tile_pool(name="keep", bufs=1))
+        psum = ctx.enter_context(tc.psum_pool(name="psum", bufs=1))
+
+        offs_t = lists.tile([P, S // 16], U16, name="offs_t")
+        par_t = lists.tile([P, S // 16], U16, name="par_t")
+        w1_raw = keep.tile([P, PACK, H], F32, name="w1_raw", align_bytes=64)
+        x_table = keep.tile([P, T], U32, name="x_table", align_bytes=64)
+        xs_table = keep.tile([P, T], U8, name="xs_table", align_bytes=64)
+        w2_raw = keep.tile([P, N], I32, name="w2_raw", align_bytes=64)
+        w2s_raw = keep.tile([P, N], U8, name="w2s_raw", align_bytes=64)
+
+        nc.gpsimd.memset(xs_table[:].bitcast(I32), 0)
+        nc.gpsimd.memset(w2s_raw[:].bitcast(I32), 0)
+        nc.sync.dma_start(offs_t[:], offs)
+        nc.sync.dma_start(w1_raw[:], w1.rearrange("(p j) c -> p j c", j=PACK))
+        nc.sync.dma_start(x_table[:].bitcast(I32), x_words[0].rearrange("p n t -> p (n t)").bitcast(I32))
+        for q in range(4):
+            nc.scalar.dma_start(xs_table[32 * q : 32 * q + 4, :].bitcast(I32), x_scales[0][4 * q : 4 * q + 4, :].bitcast(I32))
+        nc.sync.dma_start(w2_raw[:], w2_words[0].rearrange("p n t -> p (n t)").bitcast(I32))
+        nc.sync.dma_start(par_t[:], par)
+        for q in range(4):
+            nc.gpsimd.dma_start(w2s_raw[32 * q : 32 * q + 4, :].bitcast(I32), w2_scales[0][4 * q : 4 * q + 4, :].bitcast(I32))
+
+        xs = keep.tile([P, S], U8, name="xs", align_bytes=64)
+        nc.vector.tensor_copy(xs[:], xs_table[:].indirect(offs_t[:]))
+
+        w1_b = keep.tile([P, PACK * H], BF16, name="w1_b", align_bytes=64)
+        w1_dst = w1_b[:].rearrange("p (t m j) -> p m j t", t=PACK, j=PACK)
+        w1_src = w1_raw[:].rearrange("p j (m t) -> p m j t", t=PACK)
+        nc.scalar.activation(w1_dst[:, W1_SPLIT:], w1_src[:, W1_SPLIT:], ACT.Copy)
+        nc.vector.tensor_copy(w1_dst[:, :W1_SPLIT], w1_src[:, :W1_SPLIT])
+        w1_q = keep.tile([P, H], U32, name="w1_q", align_bytes=64)
+        w1_s = keep.tile([P, H], U8, name="w1_s", align_bytes=64)
+        nc.vector.quantize_mx(out=w1_q[:].bitcast(FP8X4), scales=w1_s[:], in_=w1_b[:])
+
+        xw = keep.tile([P, S], U32, name="xw", align_bytes=64)
+        for h in range(2):
+            nc.vector.tensor_copy(
+                xw[:, h * HALF : (h + 1) * HALF], x_table[:].indirect(offs_t[:, h * HALF // 16 : (h + 1) * HALF // 16])
+            )
+
+        def layer1(bank, t, cols):
+            rows = slice(t * P, (t + 1) * P)
+            nc.tensor.matmul_mx(
+                out=bank,
+                lhsT=w1_q[:, rows].bitcast(FP8X4),
+                lhsT_scale=w1_s[:, rows],
+                rhs=xw[:, cols].bitcast(FP8X4),
+                rhs_scale=xs[:, cols],
+                start=True,
+                stop=True,
+            )
+
+        y_win = [keep.tile([P, 2 * S], F32, name="y_win%d" % t, align_bytes=64) for t in range(PACK)]
+        y_dup = [keep.tile([P, S], F32, name="y_dup%d" % t, align_bytes=64) for t in range(PACK)]
+        for h in range(2):
+            cols = slice(h * HALF, (h + 1) * HALF)
+            bank = psum.tile([P, HALF], F32, name="y0_bank%d" % h)
+            layer1(bank[:], 0, cols)
+            nc.scalar.copy(y_win[0][:, cols], bank[:])
+            if h == 0:
+                nc.scalar.copy(y_dup[0][:, cols], bank[:])
+            else:
+                nc.vector.tensor_copy(y_dup[0][:, cols], bank[:])
+        for t in range(1, PACK):
+            bank = psum.tile([P, S], F32, name="y_bank%d" % t)
+            layer1(bank[:], t, slice(0, S))
+            nc.scalar.copy(y_win[t][:, :S], bank[:])
+            nc.scalar.copy(y_dup[t][:], bank[:])
+
+        w2_q = keep.tile([P, N], I32, name="w2_q", align_bytes=64)
+        nc.vector.tensor_copy(
+            w2_q[:].rearrange("p (t m) -> p m t", t=PACK), w2_raw[:].rearrange("p (m t) -> p m t", t=PACK)
+        )
+
+        w2_s = keep.tile([P, N], U8, name="w2_s", align_bytes=64)
+        nc.vector.tensor_copy(
+            w2_s[:].rearrange("p (t m) -> p m t", t=PACK), w2s_raw[:].rearrange("p (m t) -> p m t", t=PACK)
+        )
+
+        e_win = [keep.tile([P, S], F32, name="e_win%d" % t, align_bytes=64) for t in range(PACK)]
+        for t in range(PACK):
+            nc.vector.tensor_tensor(e_win[t][:], y_win[t][:].indirect(par_t[:]), y_dup[t][:], ALU.subtract)
+
+        out_words = keep.tile([P, S], U32, name="out_words", align_bytes=64)
+        out_scales = keep.tile([P, S], U8, name="out_scales", align_bytes=64)
+        out_rows = out_0.rearrange("(p t) c -> p t c", t=PACK)
+        out_word_rows = out_1[0].rearrange("p n t -> p (n t)").bitcast(I32)
+        pieces = S // PIECE
+        neg = {}
+        zb = {}
+        acc = {}
+        of = {}
+        ob = {}
+
+        def woven(ap):
+            return ap.rearrange("p (c i t) -> p c t i", i=4, t=PACK)
+
+        def planes(ap):
+            return ap.rearrange("p t (c i) -> p c t i", i=4)
+
+        def hop2(c):
+            cols = slice(c * PIECE, (c + 1) * PIECE)
+            neg[c] = keep.tile([P, PACK, PIECE], F32, name="neg%d" % c, align_bytes=64)
+            for t in range(PACK):
+                nc.vector.tensor_tensor(
+                    neg[c][:, t, :],
+                    e_win[t][:].indirect(par_t[:, c * PIECE // 16 : (c + 1) * PIECE // 16]),
+                    y_dup[t][:, cols],
+                    ALU.subtract,
+                )
+
+        def rectify(c):
+            zb[c] = keep.tile([P, PACK * PIECE], BF16, name="zb%d" % c, align_bytes=64)
+            if c < pieces - 1:
+                nc.scalar.activation(woven(zb[c][:]), planes(neg[c][:]), ACT.Relu, scale=-1.0)
+            else:
+                nc.vector.tensor_scalar(woven(zb[c][:]), planes(neg[c][:]), -1.0, 0.0, ALU.mult, ALU.max)
+
+        def layer2(c):
+            codes = keep.tile([P, PIECE], U32, name="zq%d" % c, align_bytes=64)
+            scales = keep.tile([P, PIECE], U8, name="zs%d" % c, align_bytes=64)
+            nc.vector.quantize_mx(out=codes[:].bitcast(FP8X4), scales=scales[:], in_=zb[c][:])
+            acc[c] = psum.tile([P, PACK, PIECE], F32, name="acc%d" % (c % 3))
+            for t in range(PACK):
+                rows = slice(t * P, (t + 1) * P)
+                nc.tensor.matmul_mx(
+                    out=acc[c][:, t, :],
+                    lhsT=w2_q[:, rows].bitcast(FP8X4),
+                    lhsT_scale=w2_s[:, rows],
+                    rhs=codes[:].bitcast(FP8X4),
+                    rhs_scale=scales[:],
+                    start=True,
+                    stop=True,
+                )
+
+        def store_values(c):
+            cols = slice(c * PIECE, (c + 1) * PIECE)
+            of[c] = keep.tile([P, PACK, PIECE], F32, name="of%d" % c, align_bytes=64)
+            nc.scalar.copy(of[c][:], acc[c][:])
+            nc.sync.dma_start(out_rows[:, :, cols], of[c][:])
+
+        def round_out(c):
+            ob[c] = keep.tile([P, PACK * PIECE], BF16, name="ob%d" % c, align_bytes=64)
+            if c == 0:
+                nc.scalar.copy(woven(ob[c][:]), planes(acc[c][:]))
+            else:
+                nc.vector.tensor_copy(woven(ob[c][:]), planes(of[c][:]))
+
+        def store_codes(c):
+            cols = slice(c * PIECE, (c + 1) * PIECE)
+            nc.vector.quantize_mx(out=out_words[:, cols].bitcast(FP8X4), scales=out_scales[:, cols], in_=ob[c][:])
+            nc.sync.dma_start(out_word_rows[:, cols], out_words[:, cols].bitcast(I32))
+
+        hop2(0)
+        rectify(0)
+        hop2(1)
+        rectify(1)
+        layer2(0)
+        store_values(0)
+        round_out(0)
+        hop2(2)
+        rectify(2)
+        layer2(1)
+        store_values(1)
+        hop2(3)
+        layer2(2)
+        rectify(3)
+        store_codes(0)
+        layer2(3)
+        store_values(2)
+        store_values(3)
+        for c in range(1, pieces):
+            round_out(c)
+            store_codes(c)
+        for q in range(4):
+            eng = nc.scalar if q % 2 else nc.sync
+            eng.dma_start(out_2[0][4 * q : 4 * q + 4, :].bitcast(I32), out_scales[32 * q : 32 * q + 4, :].bitcast(I32))

@@ -19,7 +19,7 @@ P = 128
 PACK = 4
 HALF = S // 2
 PIECE = 128
-W1_SPLIT = 80
+W1_SPLIT = 64
 
 
 def tile_picked_ptrjump_relu_po_kernel(
@@ -39,26 +39,26 @@ def tile_picked_ptrjump_relu_po_kernel(
         w2_raw = keep.tile([P, N], I32, name="w2_raw", align_bytes=64)
         w2s_raw = keep.tile([P, N], U8, name="w2s_raw", align_bytes=64)
 
-        nc.gpsimd.memset(xs_table[:].bitcast(I32), 0)
+        nc.vector.memset(xs_table[:].bitcast(I32), 0)
         nc.gpsimd.memset(w2s_raw[:].bitcast(I32), 0)
         nc.sync.dma_start(offs_t[:], offs)
         nc.sync.dma_start(w1_raw[:], w1.rearrange("(p j) c -> p j c", j=PACK))
+        for q in range(4):
+            nc.sync.dma_start(xs_table[32 * q : 32 * q + 4, :].bitcast(I32), x_scales[0][4 * q : 4 * q + 4, :].bitcast(I32))
         nc.sync.dma_start(x_table[:].bitcast(I32), x_words[0].rearrange("p n t -> p (n t)").bitcast(I32))
         for q in range(4):
-            nc.scalar.dma_start(xs_table[32 * q : 32 * q + 4, :].bitcast(I32), x_scales[0][4 * q : 4 * q + 4, :].bitcast(I32))
+            nc.sync.dma_start(w2s_raw[32 * q : 32 * q + 4, :].bitcast(I32), w2_scales[0][4 * q : 4 * q + 4, :].bitcast(I32))
         nc.sync.dma_start(w2_raw[:], w2_words[0].rearrange("p n t -> p (n t)").bitcast(I32))
         nc.sync.dma_start(par_t[:], par)
-        for q in range(4):
-            nc.gpsimd.dma_start(w2s_raw[32 * q : 32 * q + 4, :].bitcast(I32), w2_scales[0][4 * q : 4 * q + 4, :].bitcast(I32))
-
-        xs = keep.tile([P, S], U8, name="xs", align_bytes=64)
-        nc.vector.tensor_copy(xs[:], xs_table[:].indirect(offs_t[:]))
 
         w1_b = keep.tile([P, PACK * H], BF16, name="w1_b", align_bytes=64)
         w1_dst = w1_b[:].rearrange("p (t m j) -> p m j t", t=PACK, j=PACK)
         w1_src = w1_raw[:].rearrange("p j (m t) -> p m j t", t=PACK)
         nc.scalar.activation(w1_dst[:, W1_SPLIT:], w1_src[:, W1_SPLIT:], ACT.Copy)
         nc.vector.tensor_copy(w1_dst[:, :W1_SPLIT], w1_src[:, :W1_SPLIT])
+        xs = keep.tile([P, S], U8, name="xs", align_bytes=64)
+        nc.vector.tensor_copy(xs[:], xs_table[:].indirect(offs_t[:]))
+
         w1_q = keep.tile([P, H], U32, name="w1_q", align_bytes=64)
         w1_s = keep.tile([P, H], U8, name="w1_s", align_bytes=64)
         nc.vector.quantize_mx(out=w1_q[:].bitcast(FP8X4), scales=w1_s[:], in_=w1_b[:])
@@ -88,22 +88,19 @@ def tile_picked_ptrjump_relu_po_kernel(
             bank = psum.tile([P, HALF], F32, name="y0_bank%d" % h)
             layer1(bank[:], 0, cols)
             nc.scalar.copy(y_win[0][:, cols], bank[:])
-            if h == 0:
-                nc.scalar.copy(y_dup[0][:, cols], bank[:])
-            else:
-                nc.vector.tensor_copy(y_dup[0][:, cols], bank[:])
+            nc.scalar.copy(y_dup[0][:, cols], bank[:])
         for t in range(1, PACK):
             bank = psum.tile([P, S], F32, name="y_bank%d" % t)
             layer1(bank[:], t, slice(0, S))
             nc.scalar.copy(y_win[t][:, :S], bank[:])
             nc.scalar.copy(y_dup[t][:], bank[:])
 
-        w2_q = keep.tile([P, N], I32, name="w2_q", align_bytes=64)
+        w2_q = keep.tile([P, N], I32, name="w2_q", tag="x_table", align_bytes=64)
         nc.vector.tensor_copy(
             w2_q[:].rearrange("p (t m) -> p m t", t=PACK), w2_raw[:].rearrange("p (m t) -> p m t", t=PACK)
         )
 
-        w2_s = keep.tile([P, N], U8, name="w2_s", align_bytes=64)
+        w2_s = keep.tile([P, N], U8, name="w2_s", tag="w2_raw", align_bytes=64)
         nc.vector.tensor_copy(
             w2_s[:].rearrange("p (t m) -> p m t", t=PACK), w2s_raw[:].rearrange("p (m t) -> p m t", t=PACK)
         )
@@ -121,7 +118,7 @@ def tile_picked_ptrjump_relu_po_kernel(
         zb = {}
         acc = {}
         of = {}
-        ob = {}
+        whole = {}
 
         def woven(ap):
             return ap.rearrange("p (c i t) -> p c t i", i=4, t=PACK)
@@ -131,7 +128,8 @@ def tile_picked_ptrjump_relu_po_kernel(
 
         def hop2(c):
             cols = slice(c * PIECE, (c + 1) * PIECE)
-            neg[c] = keep.tile([P, PACK, PIECE], F32, name="neg%d" % c, align_bytes=64)
+            behind = ["neg0", "y_win3", "zb0", "zb1"][c]
+            neg[c] = keep.tile([P, PACK, PIECE], F32, name="neg%d" % c, tag=behind, align_bytes=64)
             for t in range(PACK):
                 nc.vector.tensor_tensor(
                     neg[c][:, t, :],
@@ -147,15 +145,24 @@ def tile_picked_ptrjump_relu_po_kernel(
             else:
                 nc.vector.tensor_scalar(woven(zb[c][:]), planes(neg[c][:]), -1.0, 0.0, ALU.mult, ALU.max)
 
+        last = pieces - 1
+
         def layer2(c):
             codes = keep.tile([P, PIECE], U32, name="zq%d" % c, align_bytes=64)
             scales = keep.tile([P, PIECE], U8, name="zs%d" % c, align_bytes=64)
             nc.vector.quantize_mx(out=codes[:].bitcast(FP8X4), scales=scales[:], in_=zb[c][:])
-            acc[c] = psum.tile([P, PACK, PIECE], F32, name="acc%d" % (c % 3))
+            if c < last:
+                bank = psum.tile([P, PACK, PIECE], F32, name="acc%d" % c)
+                acc[c] = [bank[:, t, :] for t in range(PACK)]
+                whole[c] = bank
+            else:
+                tags = ["y0_bank0", "y0_bank1", "y_bank1", "y_bank2"]
+                banks = [psum.tile([P, PIECE], F32, name="last%d" % t, tag=tags[t]) for t in range(PACK)]
+                acc[c] = [bank[:] for bank in banks]
             for t in range(PACK):
                 rows = slice(t * P, (t + 1) * P)
                 nc.tensor.matmul_mx(
-                    out=acc[c][:, t, :],
+                    out=acc[c][t],
                     lhsT=w2_q[:, rows].bitcast(FP8X4),
                     lhsT_scale=w2_s[:, rows],
                     rhs=codes[:].bitcast(FP8X4),
@@ -167,42 +174,44 @@ def tile_picked_ptrjump_relu_po_kernel(
         def store_values(c):
             cols = slice(c * PIECE, (c + 1) * PIECE)
             of[c] = keep.tile([P, PACK, PIECE], F32, name="of%d" % c, align_bytes=64)
-            nc.scalar.copy(of[c][:], acc[c][:])
+            if c < last:
+                nc.scalar.copy(of[c][:], whole[c][:])
+            else:
+                for t in range(PACK):
+                    nc.scalar.copy(of[c][:, t, :], acc[c][t])
             nc.sync.dma_start(out_rows[:, :, cols], of[c][:])
 
-        def round_out(c):
-            ob[c] = keep.tile([P, PACK * PIECE], BF16, name="ob%d" % c, align_bytes=64)
-            if c == 0:
-                nc.scalar.copy(woven(ob[c][:]), planes(acc[c][:]))
-            else:
-                nc.vector.tensor_copy(woven(ob[c][:]), planes(of[c][:]))
+        def quantise_out(src, cols):
+            nc.vector.quantize_mx(out=out_words[:, cols].bitcast(FP8X4), scales=out_scales[:, cols], in_=src)
 
-        def store_codes(c):
-            cols = slice(c * PIECE, (c + 1) * PIECE)
-            nc.vector.quantize_mx(out=out_words[:, cols].bitcast(FP8X4), scales=out_scales[:, cols], in_=ob[c][:])
-            nc.sync.dma_start(out_word_rows[:, cols], out_words[:, cols].bitcast(I32))
-
+        ob0 = keep.tile([P, PACK * PIECE], BF16, name="ob0", align_bytes=64)
         hop2(0)
         rectify(0)
         hop2(1)
         rectify(1)
         layer2(0)
         store_values(0)
-        round_out(0)
         hop2(2)
         rectify(2)
+        nc.scalar.copy(woven(ob0[:]), planes(whole[0][:]))
         layer2(1)
         store_values(1)
         hop2(3)
         layer2(2)
         rectify(3)
-        store_codes(0)
+        quantise_out(ob0[:], slice(0, PIECE))
         layer2(3)
         store_values(2)
         store_values(3)
-        for c in range(1, pieces):
-            round_out(c)
-            store_codes(c)
+        ob12 = keep.tile([P, 2 * PACK * PIECE], BF16, name="ob12", tag="zb3", align_bytes=64)
+        for c in (1, 2):
+            nc.vector.tensor_copy(woven(ob12[:, (c - 1) * PACK * PIECE : c * PACK * PIECE]), planes(of[c][:]))
+        quantise_out(ob12[:], slice(PIECE, last * PIECE))
+        nc.sync.dma_start(out_word_rows[:, : last * PIECE], out_words[:, : last * PIECE].bitcast(I32))
+        ob3 = keep.tile([P, PACK * PIECE], BF16, name="ob3", align_bytes=64)
+        nc.vector.tensor_copy(woven(ob3[:]), planes(of[last][:]))
+        quantise_out(ob3[:], slice(last * PIECE, S))
+        nc.sync.dma_start(out_word_rows[:, last * PIECE :], out_words[:, last * PIECE :].bitcast(I32))
         for q in range(4):
-            eng = nc.scalar if q % 2 else nc.sync
+            eng = nc.sync if q % 2 else nc.scalar
             eng.dma_start(out_2[0][4 * q : 4 * q + 4, :].bitcast(I32), out_scales[32 * q : 32 * q + 4, :].bitcast(I32))

@@ -44,10 +44,10 @@ def tile_picked_ptrjump_relu_po_kernel(
         nc.sync.dma_start(offs_t[:], offs)
         nc.sync.dma_start(w1_raw[:], w1.rearrange("(p j) c -> p j c", j=PACK))
         for q in range(4):
-            nc.sync.dma_start(xs_table[32 * q : 32 * q + 4, :].bitcast(I32), x_scales[0][4 * q : 4 * q + 4, :].bitcast(I32))
+            nc.sync.dma_start(xs_table[q:P:32, :].bitcast(I32), x_scales[0][q:16:4, :].bitcast(I32))
         nc.sync.dma_start(x_table[:].bitcast(I32), x_words[0].rearrange("p n t -> p (n t)").bitcast(I32))
         for q in range(4):
-            nc.sync.dma_start(w2s_raw[32 * q : 32 * q + 4, :].bitcast(I32), w2_scales[0][4 * q : 4 * q + 4, :].bitcast(I32))
+            nc.sync.dma_start(w2s_raw[q:P:32, :].bitcast(I32), w2_scales[0][q:16:4, :].bitcast(I32))
         nc.sync.dma_start(w2_raw[:], w2_words[0].rearrange("p n t -> p (n t)").bitcast(I32))
         nc.sync.dma_start(par_t[:], par)
 
@@ -106,7 +106,11 @@ def tile_picked_ptrjump_relu_po_kernel(
         )
 
         e_win = [keep.tile([P, S], F32, name="e_win%d" % t, align_bytes=64) for t in range(PACK)]
-        for t in range(PACK):
+        for h in range(2):
+            cols = slice(h * HALF, (h + 1) * HALF)
+            half_list = par_t[:, h * HALF // 16 : (h + 1) * HALF // 16]
+            nc.vector.tensor_tensor(e_win[0][:, cols], y_win[0][:].indirect(half_list), y_dup[0][:, cols], ALU.subtract)
+        for t in range(1, PACK):
             nc.vector.tensor_tensor(e_win[t][:], y_win[t][:].indirect(par_t[:]), y_dup[t][:], ALU.subtract)
 
         out_words = keep.tile([P, S], U32, name="out_words", align_bytes=64)
@@ -126,31 +130,40 @@ def tile_picked_ptrjump_relu_po_kernel(
         def planes(ap):
             return ap.rearrange("p t (c i) -> p c t i", i=4)
 
-        def hop2(c):
+        def room(c):
+            behind = ["neg0", "y_win3", "neg0", "y_win3"][c]
+            neg[c] = keep.tile([P, (PACK + 1) * PIECE], F32, name="neg%d" % c, tag=behind, align_bytes=64)
+
+        def hop2(c, tiles):
             cols = slice(c * PIECE, (c + 1) * PIECE)
-            behind = ["neg0", "y_win3", "zb0", "zb1"][c]
-            neg[c] = keep.tile([P, PACK, PIECE], F32, name="neg%d" % c, tag=behind, align_bytes=64)
-            for t in range(PACK):
+            for t in tiles:
                 nc.vector.tensor_tensor(
-                    neg[c][:, t, :],
+                    neg[c][:, t * PIECE : (t + 1) * PIECE],
                     e_win[t][:].indirect(par_t[:, c * PIECE // 16 : (c + 1) * PIECE // 16]),
                     y_dup[t][:, cols],
                     ALU.subtract,
                 )
 
         def rectify(c):
-            zb[c] = keep.tile([P, PACK * PIECE], BF16, name="zb%d" % c, align_bytes=64)
+            src = planes(neg[c][:, : PACK * PIECE].rearrange("p (t n) -> p t n", t=PACK))
             if c < pieces - 1:
-                nc.scalar.activation(woven(zb[c][:]), planes(neg[c][:]), ACT.Relu, scale=-1.0)
+                if c == pieces - 2:
+                    zb[c] = neg[c + 1][:, (PACK - 1) * PIECE :].bitcast(BF16)
+                else:
+                    own = keep.tile([P, PACK * PIECE], BF16, name="zb%d" % c, align_bytes=64)
+                    zb[c] = own[:]
+                nc.scalar.activation(woven(zb[c]), src, ACT.Relu, scale=-1.0)
             else:
-                nc.vector.tensor_scalar(woven(zb[c][:]), planes(neg[c][:]), -1.0, 0.0, ALU.mult, ALU.max)
+                zb3 = keep.tile([P, PACK * PIECE], BF16, name="zb3", align_bytes=64)
+                zb[c] = zb3[:]
+                nc.vector.tensor_scalar(woven(zb[c]), src, -1.0, 0.0, ALU.mult, ALU.max)
 
         last = pieces - 1
 
         def layer2(c):
             codes = keep.tile([P, PIECE], U32, name="zq%d" % c, align_bytes=64)
             scales = keep.tile([P, PIECE], U8, name="zs%d" % c, align_bytes=64)
-            nc.vector.quantize_mx(out=codes[:].bitcast(FP8X4), scales=scales[:], in_=zb[c][:])
+            nc.vector.quantize_mx(out=codes[:].bitcast(FP8X4), scales=scales[:], in_=zb[c])
             if c < last:
                 bank = psum.tile([P, PACK, PIECE], F32, name="acc%d" % c)
                 acc[c] = [bank[:, t, :] for t in range(PACK)]
@@ -185,20 +198,25 @@ def tile_picked_ptrjump_relu_po_kernel(
             nc.vector.quantize_mx(out=out_words[:, cols].bitcast(FP8X4), scales=out_scales[:, cols], in_=src)
 
         ob0 = keep.tile([P, PACK * PIECE], BF16, name="ob0", align_bytes=64)
-        hop2(0)
+        room(0)
+        hop2(0, range(PACK))
         rectify(0)
-        hop2(1)
+        room(1)
+        hop2(1, range(PACK))
         rectify(1)
         layer2(0)
         store_values(0)
-        hop2(2)
-        rectify(2)
-        nc.scalar.copy(woven(ob0[:]), planes(whole[0][:]))
+        room(2)
+        hop2(2, range(PACK))
         layer2(1)
+        room(3)
+        rectify(2)
+        nc.scalar.copy(ob0[:].rearrange("p (n t) -> p n t", t=PACK), whole[0][:].rearrange("p t n -> p n t"))
         store_values(1)
-        hop2(3)
+        hop2(3, range(PACK - 1))
         layer2(2)
-        rectify(3)
+        hop2(3, [PACK - 1])
+        rectify(last)
         quantise_out(ob0[:], slice(0, PIECE))
         layer2(3)
         store_values(2)
@@ -211,7 +229,7 @@ def tile_picked_ptrjump_relu_po_kernel(
         ob3 = keep.tile([P, PACK * PIECE], BF16, name="ob3", align_bytes=64)
         nc.vector.tensor_copy(woven(ob3[:]), planes(of[last][:]))
         quantise_out(ob3[:], slice(last * PIECE, S))
-        nc.sync.dma_start(out_word_rows[:, last * PIECE :], out_words[:, last * PIECE :].bitcast(I32))
+        nc.scalar.dma_start(out_word_rows[:, last * PIECE :], out_words[:, last * PIECE :].bitcast(I32))
         for q in range(4):
-            eng = nc.sync if q % 2 else nc.scalar
-            eng.dma_start(out_2[0][4 * q : 4 * q + 4, :].bitcast(I32), out_scales[32 * q : 32 * q + 4, :].bitcast(I32))
+            eng = nc.scalar if q == 3 else nc.sync
+            eng.dma_start(out_2[0][q:16:4, :].bitcast(I32), out_scales[q:P:32, :].bitcast(I32))

@@ -82,7 +82,9 @@ def tile_picked_ptrjump_relu_po_kernel(
             )
 
         y_win = [keep.tile([P, 2 * S], F32, name="y_win%d" % t, align_bytes=64) for t in range(PACK)]
-        y_dup = [keep.tile([P, S], F32, name="y_dup%d" % t, align_bytes=64) for t in range(PACK)]
+        ring = keep.tile([P, (2 * PACK + 1) * PIECE], F32, name="ring", align_bytes=64)
+        y_dup = [keep.tile([P, S], F32, name="y_dup%d" % t, align_bytes=64)[:] for t in range(PACK - 1)]
+        y_dup.append(ring[:, (PACK + 1) * PIECE :])
         for h in range(2):
             cols = slice(h * HALF, (h + 1) * HALF)
             bank = psum.tile([P, HALF], F32, name="y0_bank%d" % h)
@@ -93,7 +95,7 @@ def tile_picked_ptrjump_relu_po_kernel(
             bank = psum.tile([P, S], F32, name="y_bank%d" % t)
             layer1(bank[:], t, slice(0, S))
             nc.scalar.copy(y_win[t][:, :S], bank[:])
-            nc.scalar.copy(y_dup[t][:], bank[:])
+            nc.scalar.copy(y_dup[t], bank[:])
 
         w2_q = keep.tile([P, N], I32, name="w2_q", tag="x_table", align_bytes=64)
         nc.vector.tensor_copy(
@@ -110,15 +112,12 @@ def tile_picked_ptrjump_relu_po_kernel(
             cols = slice(h * HALF, (h + 1) * HALF)
             half_list = par_t[:, h * HALF // 16 : (h + 1) * HALF // 16]
             nc.vector.tensor_tensor(e_win[0][:, cols], y_win[0][:].indirect(half_list), y_dup[0][:, cols], ALU.subtract)
-        for t in range(1, PACK):
-            nc.vector.tensor_tensor(e_win[t][:], y_win[t][:].indirect(par_t[:]), y_dup[t][:], ALU.subtract)
 
         out_words = keep.tile([P, S], U32, name="out_words", align_bytes=64)
         out_scales = keep.tile([P, S], U8, name="out_scales", align_bytes=64)
         out_rows = out_0.rearrange("(p t) c -> p t c", t=PACK)
         out_word_rows = out_1[0].rearrange("p n t -> p (n t)").bitcast(I32)
         pieces = S // PIECE
-        neg = {}
         zb = {}
         acc = {}
         of = {}
@@ -130,32 +129,30 @@ def tile_picked_ptrjump_relu_po_kernel(
         def planes(ap):
             return ap.rearrange("p t (c i) -> p c t i", i=4)
 
-        def room(c):
-            behind = ["neg0", "y_win3", "neg0", "y_win3"][c]
-            neg[c] = keep.tile([P, (PACK + 1) * PIECE], F32, name="neg%d" % c, tag=behind, align_bytes=64)
+        def slots(c):
+            first = [PIECE // 2, PACK * PIECE, 0, PACK * PIECE][c]
+            return ring[:, first : first + PACK * PIECE]
 
         def hop2(c, tiles):
             cols = slice(c * PIECE, (c + 1) * PIECE)
             for t in tiles:
                 nc.vector.tensor_tensor(
-                    neg[c][:, t * PIECE : (t + 1) * PIECE],
+                    slots(c)[:, t * PIECE : (t + 1) * PIECE],
                     e_win[t][:].indirect(par_t[:, c * PIECE // 16 : (c + 1) * PIECE // 16]),
-                    y_dup[t][:, cols],
+                    y_win[t][:, cols],
                     ALU.subtract,
                 )
 
+        zb3_room = ring[:, : 2 * PIECE].bitcast(BF16)
+
         def rectify(c):
-            src = planes(neg[c][:, : PACK * PIECE].rearrange("p (t n) -> p t n", t=PACK))
+            src = planes(slots(c).rearrange("p (t n) -> p t n", t=PACK))
             if c < pieces - 1:
-                if c == pieces - 2:
-                    zb[c] = neg[c + 1][:, (PACK - 1) * PIECE :].bitcast(BF16)
-                else:
-                    own = keep.tile([P, PACK * PIECE], BF16, name="zb%d" % c, align_bytes=64)
-                    zb[c] = own[:]
+                own = keep.tile([P, PACK * PIECE], BF16, name="zb%d" % c, align_bytes=64)
+                zb[c] = own[:]
                 nc.scalar.activation(woven(zb[c]), src, ACT.Relu, scale=-1.0)
             else:
-                zb3 = keep.tile([P, PACK * PIECE], BF16, name="zb3", align_bytes=64)
-                zb[c] = zb3[:]
+                zb[c] = zb3_room
                 nc.vector.tensor_scalar(woven(zb[c]), src, -1.0, 0.0, ALU.mult, ALU.max)
 
         last = pieces - 1
@@ -197,39 +194,38 @@ def tile_picked_ptrjump_relu_po_kernel(
         def quantise_out(src, cols):
             nc.vector.quantize_mx(out=out_words[:, cols].bitcast(FP8X4), scales=out_scales[:, cols], in_=src)
 
-        ob0 = keep.tile([P, PACK * PIECE], BF16, name="ob0", align_bytes=64)
-        room(0)
+        for t in range(1, PACK):
+            nc.vector.tensor_tensor(e_win[t][:], y_win[t][:].indirect(par_t[:]), y_dup[t], ALU.subtract)
         hop2(0, range(PACK))
         rectify(0)
-        room(1)
-        hop2(1, range(PACK))
-        rectify(1)
+        hop2(1, range(1, PACK))
         layer2(0)
+        hop2(1, [0])
+        rectify(1)
         store_values(0)
-        room(2)
         hop2(2, range(PACK))
-        layer2(1)
-        room(3)
         rectify(2)
-        nc.scalar.copy(ob0[:].rearrange("p (n t) -> p n t", t=PACK), whole[0][:].rearrange("p t n -> p n t"))
+        layer2(1)
         store_values(1)
-        hop2(3, range(PACK - 1))
+        hop2(3, range(PACK))
         layer2(2)
-        hop2(3, [PACK - 1])
+        ob0 = ring[:, 2 * PIECE : PACK * PIECE].bitcast(BF16)
+        ob1 = keep.tile([P, PACK * PIECE], BF16, name="ob1", align_bytes=64)
+        ob23 = keep.tile([P, 2 * PACK * PIECE], BF16, name="ob23", align_bytes=64)
+        nc.scalar.copy(ob0.rearrange("p (n t) -> p n t", t=PACK), whole[0][:].rearrange("p t n -> p n t"))
         rectify(last)
-        quantise_out(ob0[:], slice(0, PIECE))
+        nc.vector.tensor_copy(woven(ob1[:]), planes(of[1][:]))
         layer2(3)
+        quantise_out(ob1[:], slice(PIECE, HALF))
+        quantise_out(ob0, slice(0, PIECE))
+        nc.sync.dma_start(out_word_rows[:, :HALF], out_words[:, :HALF].bitcast(I32))
         store_values(2)
         store_values(3)
-        ob12 = keep.tile([P, 2 * PACK * PIECE], BF16, name="ob12", tag="zb3", align_bytes=64)
-        for c in (1, 2):
-            nc.vector.tensor_copy(woven(ob12[:, (c - 1) * PACK * PIECE : c * PACK * PIECE]), planes(of[c][:]))
-        quantise_out(ob12[:], slice(PIECE, last * PIECE))
-        nc.sync.dma_start(out_word_rows[:, : last * PIECE], out_words[:, : last * PIECE].bitcast(I32))
-        ob3 = keep.tile([P, PACK * PIECE], BF16, name="ob3", align_bytes=64)
-        nc.vector.tensor_copy(woven(ob3[:]), planes(of[last][:]))
-        quantise_out(ob3[:], slice(last * PIECE, S))
-        nc.scalar.dma_start(out_word_rows[:, last * PIECE :], out_words[:, last * PIECE :].bitcast(I32))
+        for c in (2, 3):
+            nc.vector.tensor_copy(woven(ob23[:, (c - 2) * PACK * PIECE : (c - 1) * PACK * PIECE]), planes(of[c][:]))
+        for c in (2, 3):
+            quantise_out(ob23[:, (c - 2) * PACK * PIECE : (c - 1) * PACK * PIECE], slice(c * PIECE, (c + 1) * PIECE))
+        nc.scalar.dma_start(out_word_rows[:, HALF:], out_words[:, HALF:].bitcast(I32))
         for q in range(4):
             eng = nc.scalar if q == 3 else nc.sync
             eng.dma_start(out_2[0][q:16:4, :].bitcast(I32), out_scales[q:P:32, :].bitcast(I32))

@@ -181,6 +181,18 @@ def tile_picked_ptrjump_relu_po_kernel(
                     stop=True,
                 )
 
+            if c < 2:
+                idle = psum.tile([P, S], F32, name="idle%d" % c, tag="y_bank3")
+                nc.tensor.matmul_mx(
+                    out=idle[:],
+                    lhsT=codes[:].bitcast(FP8X4),
+                    lhsT_scale=scales[:],
+                    rhs=xw[:].bitcast(FP8X4),
+                    rhs_scale=xs[:],
+                    start=True,
+                    stop=True,
+                )
+
         def store_values(c):
             cols = slice(c * PIECE, (c + 1) * PIECE)
             of[c] = keep.tile([P, PACK, PIECE], F32, name="of%d" % c, align_bytes=64)

@@ -19,7 +19,6 @@ P = 128
 PACK = 4
 HALF = S // 2
 PIECE = 128
-W1_SPLIT = 64
 
 
 def tile_picked_ptrjump_relu_po_kernel(
@@ -36,38 +35,67 @@ def tile_picked_ptrjump_relu_po_kernel(
         w1_raw = keep.tile([P, PACK, H], F32, name="w1_raw", align_bytes=64)
         x_table = keep.tile([P, T], U32, name="x_table", align_bytes=64)
         xs_table = keep.tile([P, T], U8, name="xs_table", align_bytes=64)
-        w2_raw = keep.tile([P, N], I32, name="w2_raw", align_bytes=64)
         w2s_raw = keep.tile([P, N], U8, name="w2s_raw", align_bytes=64)
 
-        nc.vector.memset(xs_table[:].bitcast(I32), 0)
-        nc.gpsimd.memset(w2s_raw[:].bitcast(I32), 0)
+        xs = keep.tile([P, S], U8, name="xs", align_bytes=64)
+        w2_s = keep.tile([P, N], U8, name="w2_s", align_bytes=64)
+        nc.sync.dma_start(xs_table[16:32, :].bitcast(I32), x_scales[0].bitcast(I32))
+        for lo, hi in ((0, 16), (32, 64), (64, P)):
+            nc.vector.memset(xs_table[lo:hi, :].bitcast(I32), 0)
+        nc.gpsimd.memset(xs[:].bitcast(I32), 0)
+        for lo, hi in ((0, 16), (32, 64), (64, P)):
+            nc.gpsimd.memset(w2s_raw[lo:hi, :].bitcast(I32), 0)
+        nc.gpsimd.memset(w2_s[:].bitcast(I32), 0)
         nc.sync.dma_start(offs_t[:], offs)
-        nc.sync.dma_start(w1_raw[:], w1.rearrange("(p j) c -> p j c", j=PACK))
-        for q in range(4):
-            nc.sync.dma_start(xs_table[q:P:32, :].bitcast(I32), x_scales[0][q:16:4, :].bitcast(I32))
         nc.sync.dma_start(x_table[:].bitcast(I32), x_words[0].rearrange("p n t -> p (n t)").bitcast(I32))
-        for q in range(4):
-            nc.sync.dma_start(w2s_raw[q:P:32, :].bitcast(I32), w2_scales[0][q:16:4, :].bitcast(I32))
-        nc.sync.dma_start(w2_raw[:], w2_words[0].rearrange("p n t -> p (n t)").bitcast(I32))
+        nc.sync.dma_start(w2s_raw[16:32, :].bitcast(I32), w2_scales[0].bitcast(I32))
+        nc.sync.dma_start(w1_raw[:], w1.rearrange("(p j) c -> p j c", j=PACK))
         nc.sync.dma_start(par_t[:], par)
 
-        w1_b = keep.tile([P, PACK * H], BF16, name="w1_b", align_bytes=64)
-        w1_dst = w1_b[:].rearrange("p (t m j) -> p m j t", t=PACK, j=PACK)
-        w1_src = w1_raw[:].rearrange("p j (m t) -> p m j t", t=PACK)
-        nc.scalar.activation(w1_dst[:, W1_SPLIT:], w1_src[:, W1_SPLIT:], ACT.Copy)
-        nc.vector.tensor_copy(w1_dst[:, :W1_SPLIT], w1_src[:, :W1_SPLIT])
-        xs = keep.tile([P, S], U8, name="xs", align_bytes=64)
-        nc.vector.tensor_copy(xs[:], xs_table[:].indirect(offs_t[:]))
+        def move_rows(plane, spread):
+            for r in range(4):
+                nc.sync.dma_start(plane[r:P:32, :].bitcast(I32), spread[16 + r : 32 : 4, :].bitcast(I32))
 
-        w1_q = keep.tile([P, H], U32, name="w1_q", align_bytes=64)
-        w1_s = keep.tile([P, H], U8, name="w1_s", align_bytes=64)
-        nc.vector.quantize_mx(out=w1_q[:].bitcast(FP8X4), scales=w1_s[:], in_=w1_b[:])
+        xs_spread = keep.tile([P, S], U8, name="xs_spread", align_bytes=64)
+        nc.vector.tensor_copy(xs_spread[:], xs_table[:].indirect(offs_t[:]))
+        move_rows(xs, xs_spread)
+        w2_raw = keep.tile([P, N], I32, name="w2_raw", tag="xs_table", align_bytes=64)
+        nc.sync.dma_start(w2_raw[:], w2_words[0].rearrange("p n t -> p (n t)").bitcast(I32))
 
         xw = keep.tile([P, S], U32, name="xw", align_bytes=64)
-        for h in range(2):
-            nc.vector.tensor_copy(
-                xw[:, h * HALF : (h + 1) * HALF], x_table[:].indirect(offs_t[:, h * HALF // 16 : (h + 1) * HALF // 16])
-            )
+        nc.vector.tensor_copy(xw[:], x_table[:].indirect(offs_t[:]))
+
+        w2s_spread = keep.tile([P, N], U8, name="w2s_spread", align_bytes=64)
+        nc.vector.tensor_copy(
+            w2s_spread[:].rearrange("p (t m) -> p m t", t=PACK), w2s_raw[:].rearrange("p (m t) -> p m t", t=PACK)
+        )
+        move_rows(w2_s, w2s_spread)
+
+        w1_src = w1_raw[:].rearrange("p j (m t) -> p m j t", t=PACK)
+        w1_q = keep.tile([P, H], U32, name="w1_q", align_bytes=64)
+        w1_s = keep.tile([P, H], U8, name="w1_s", align_bytes=64)
+        w1_b = [keep.tile([P, 2 * H], BF16, name="w1_b%d" % u, align_bytes=64) for u in range(2)]
+        w1_dst = [w1_b[u][:].rearrange("p (t m j) -> p m j t", t=2, j=PACK) for u in range(2)]
+
+        def round_w1(engine, u, lo, hi):
+            src = w1_src[:, lo:hi, :, 2 * u : 2 * u + 2]
+            if engine == "scalar":
+                nc.scalar.activation(w1_dst[u][:, lo:hi], src, ACT.Copy)
+            else:
+                nc.vector.tensor_copy(w1_dst[u][:, lo:hi], src)
+
+        round_w1("scalar", 0, 96, P)
+        round_w1("vector", 0, 0, 96)
+        round_w1("scalar", 1, 56, P)
+        round_w1("vector", 1, 0, 56)
+
+        def quantise_w1(first, count):
+            cols = slice(first * P, (first + count) * P)
+            src = w1_b[first // 2][:, (first % 2) * H : (first % 2 + count) * H]
+            nc.vector.quantize_mx(out=w1_q[:, cols].bitcast(FP8X4), scales=w1_s[:, cols], in_=src)
+
+        quantise_w1(0, 1)
+        quantise_w1(1, 1)
 
         def layer1(bank, t, cols):
             rows = slice(t * P, (t + 1) * P)
@@ -81,31 +109,34 @@ def tile_picked_ptrjump_relu_po_kernel(
                 stop=True,
             )
 
+        w2_q = keep.tile([P, N], I32, name="w2_q", tag="x_table", align_bytes=64)
+        nc.vector.tensor_copy(
+            w2_q[:].rearrange("p (t m) -> p m t", t=PACK), w2_raw[:].rearrange("p (m t) -> p m t", t=PACK)
+        )
+
         y_win = [keep.tile([P, 2 * S], F32, name="y_win%d" % t, align_bytes=64) for t in range(PACK)]
         ring = keep.tile([P, (2 * PACK + 1) * PIECE], F32, name="ring", align_bytes=64)
         y_dup = [keep.tile([P, S], F32, name="y_dup%d" % t, align_bytes=64)[:] for t in range(PACK - 1)]
         y_dup.append(ring[:, (PACK + 1) * PIECE :])
-        for h in range(2):
-            cols = slice(h * HALF, (h + 1) * HALF)
-            bank = psum.tile([P, HALF], F32, name="y0_bank%d" % h)
+        for part, (first, width, tag) in enumerate([(0, HALF, "y0_bank0"), (HALF, PIECE, "y0_bank1"), (HALF + PIECE, PIECE, "acc2")]):
+            cols = slice(first, first + width)
+            bank = psum.tile([P, width], F32, name="y0_part%d" % part, tag=tag)
             layer1(bank[:], 0, cols)
-            nc.scalar.copy(y_win[0][:, cols], bank[:])
+            if part == 0:
+                nc.scalar.copy(y_win[0][:, cols], bank[:])
+            else:
+                nc.vector.tensor_copy(y_win[0][:, cols], bank[:])
             nc.scalar.copy(y_dup[0][:, cols], bank[:])
+        quantise_w1(2, 2)
         for t in range(1, PACK):
             bank = psum.tile([P, S], F32, name="y_bank%d" % t)
             layer1(bank[:], t, slice(0, S))
             nc.scalar.copy(y_win[t][:, :S], bank[:])
             nc.scalar.copy(y_dup[t], bank[:])
 
-        w2_q = keep.tile([P, N], I32, name="w2_q", tag="x_table", align_bytes=64)
-        nc.vector.tensor_copy(
-            w2_q[:].rearrange("p (t m) -> p m t", t=PACK), w2_raw[:].rearrange("p (m t) -> p m t", t=PACK)
-        )
-
-        w2_s = keep.tile([P, N], U8, name="w2_s", tag="w2_raw", align_bytes=64)
-        nc.vector.tensor_copy(
-            w2_s[:].rearrange("p (t m) -> p m t", t=PACK), w2s_raw[:].rearrange("p (m t) -> p m t", t=PACK)
-        )
+        y_late = keep.tile([P, (PACK - 1) * PIECE], F32, name="y_late", tag="w1_q", align_bytes=64)
+        for t in range(PACK - 1):
+            nc.scalar.copy(y_late[:, t * PIECE : (t + 1) * PIECE], y_win[t][:, :PIECE])
 
         e_win = [keep.tile([P, S], F32, name="e_win%d" % t, align_bytes=64) for t in range(PACK)]
         for h in range(2):
@@ -139,7 +170,7 @@ def tile_picked_ptrjump_relu_po_kernel(
                 nc.vector.tensor_tensor(
                     slots(c)[:, t * PIECE : (t + 1) * PIECE],
                     e_win[t][:].indirect(par_t[:, c * PIECE // 16 : (c + 1) * PIECE // 16]),
-                    y_win[t][:, cols],
+                    y_late[:, t * PIECE : (t + 1) * PIECE] if c == 0 and t < PACK - 1 else y_win[t][:, cols],
                     ALU.subtract,
                 )
 

@@ -115,9 +115,9 @@ def tile_picked_ptrjump_relu_po_kernel(
         )
 
         y_win = [keep.tile([P, 2 * S], F32, name="y_win%d" % t, align_bytes=64) for t in range(PACK)]
-        ring = keep.tile([P, (2 * PACK + 1) * PIECE], F32, name="ring", align_bytes=64)
+        ring = keep.tile([P, 2 * PACK * PIECE], F32, name="ring", align_bytes=64)
         y_dup = [keep.tile([P, S], F32, name="y_dup%d" % t, align_bytes=64)[:] for t in range(PACK - 1)]
-        y_dup.append(ring[:, (PACK + 1) * PIECE :])
+        y_dup.append(ring[:, PACK * PIECE :])
         for part, (first, width, tag) in enumerate([(0, HALF, "y0_bank0"), (HALF, PIECE, "y0_bank1"), (HALF + PIECE, PIECE, "acc2")]):
             cols = slice(first, first + width)
             bank = psum.tile([P, width], F32, name="y0_part%d" % part, tag=tag)
@@ -161,7 +161,7 @@ def tile_picked_ptrjump_relu_po_kernel(
             return ap.rearrange("p t (c i) -> p c t i", i=4)
 
         def slots(c):
-            first = [PIECE // 2, PACK * PIECE, 0, PACK * PIECE][c]
+            first = (c % 2) * PACK * PIECE
             return ring[:, first : first + PACK * PIECE]
 
         def hop2(c, tiles):
@@ -179,7 +179,7 @@ def tile_picked_ptrjump_relu_po_kernel(
         def rectify(c):
             src = planes(slots(c).rearrange("p (t n) -> p t n", t=PACK))
             if c < pieces - 1:
-                own = keep.tile([P, PACK * PIECE], BF16, name="zb%d" % c, align_bytes=64)
+                own = keep.tile([P, PACK * PIECE], BF16, name="zb%d" % c, tag="zq0" if c == 2 else "zb%d" % c, align_bytes=64)
                 zb[c] = own[:]
                 nc.scalar.activation(woven(zb[c]), src, ACT.Relu, scale=-1.0)
             else:
@@ -241,26 +241,25 @@ def tile_picked_ptrjump_relu_po_kernel(
             nc.vector.tensor_tensor(e_win[t][:], y_win[t][:].indirect(par_t[:]), y_dup[t], ALU.subtract)
         hop2(0, range(PACK))
         rectify(0)
-        hop2(1, range(1, PACK))
-        layer2(0)
-        hop2(1, [0])
+        hop2(1, range(PACK))
         rectify(1)
+        layer2(0)
         store_values(0)
         hop2(2, range(PACK))
         rectify(2)
         layer2(1)
-        store_values(1)
-        hop2(3, range(PACK))
-        layer2(2)
         ob0 = ring[:, 2 * PIECE : PACK * PIECE].bitcast(BF16)
         ob1 = keep.tile([P, PACK * PIECE], BF16, name="ob1", align_bytes=64)
         ob23 = keep.tile([P, 2 * PACK * PIECE], BF16, name="ob23", align_bytes=64)
         nc.scalar.copy(ob0.rearrange("p (n t) -> p n t", t=PACK), whole[0][:].rearrange("p t n -> p n t"))
+        store_values(1)
+        hop2(3, range(PACK))
+        layer2(2)
         rectify(last)
-        nc.vector.tensor_copy(woven(ob1[:]), planes(of[1][:]))
-        layer2(3)
-        quantise_out(ob1[:], slice(PIECE, HALF))
         quantise_out(ob0, slice(0, PIECE))
+        layer2(3)
+        nc.vector.tensor_copy(woven(ob1[:]), planes(of[1][:]))
+        quantise_out(ob1[:], slice(PIECE, HALF))
         nc.sync.dma_start(out_word_rows[:, :HALF], out_words[:, :HALF].bitcast(I32))
         store_values(2)
         store_values(3)

@@ -85,16 +85,20 @@ def tile_picked_ptrjump_relu_po_kernel(
                 nc.vector.tensor_copy(w1_dst[u][:, lo:hi], src)
 
         round_w1("scalar", 0, 96, P)
-        round_w1("vector", 0, 0, 96)
+        round_w1("vector", 0, 0, 64)
+        round_w1("vector", 0, 64, 96)
         round_w1("scalar", 1, 56, P)
-        round_w1("vector", 1, 0, 56)
 
         def quantise_w1(first, count):
             cols = slice(first * P, (first + count) * P)
             src = w1_b[first // 2][:, (first % 2) * H : (first % 2 + count) * H]
             nc.vector.quantize_mx(out=w1_q[:, cols].bitcast(FP8X4), scales=w1_s[:, cols], in_=src)
 
-        quantise_w1(0, 1)
+        for lo in (0, 64):
+            nc.vector.quantize_mx(
+                out=w1_q[:, lo : lo + 64].bitcast(FP8X4), scales=w1_s[:, lo : lo + 64], in_=w1_b[0][:, 4 * lo : 4 * lo + 256]
+            )
+        round_w1("vector", 1, 0, 56)
         quantise_w1(1, 1)
 
         def layer1(bank, t, cols):
@@ -248,17 +252,17 @@ def tile_picked_ptrjump_relu_po_kernel(
         hop2(2, range(PACK))
         rectify(2)
         layer2(1)
-        ob0 = ring[:, 2 * PIECE : PACK * PIECE].bitcast(BF16)
+        ob0 = keep.tile([P, PACK * PIECE], BF16, name="ob0", tag="zq1", align_bytes=64)[:]
         ob1 = keep.tile([P, PACK * PIECE], BF16, name="ob1", align_bytes=64)
         ob23 = keep.tile([P, 2 * PACK * PIECE], BF16, name="ob23", align_bytes=64)
-        nc.scalar.copy(ob0.rearrange("p (n t) -> p n t", t=PACK), whole[0][:].rearrange("p t n -> p n t"))
         store_values(1)
+        nc.scalar.copy(ob0.rearrange("p (n t) -> p n t", t=PACK), whole[0][:].rearrange("p t n -> p n t"))
         hop2(3, range(PACK))
         layer2(2)
         rectify(last)
-        quantise_out(ob0, slice(0, PIECE))
         layer2(3)
         nc.vector.tensor_copy(woven(ob1[:]), planes(of[1][:]))
+        quantise_out(ob0, slice(0, PIECE))
         quantise_out(ob1[:], slice(PIECE, HALF))
         nc.sync.dma_start(out_word_rows[:, :HALF], out_words[:, :HALF].bitcast(I32))
         store_values(2)
@@ -267,7 +271,7 @@ def tile_picked_ptrjump_relu_po_kernel(
             nc.vector.tensor_copy(woven(ob23[:, (c - 2) * PACK * PIECE : (c - 1) * PACK * PIECE]), planes(of[c][:]))
         for c in (2, 3):
             quantise_out(ob23[:, (c - 2) * PACK * PIECE : (c - 1) * PACK * PIECE], slice(c * PIECE, (c + 1) * PIECE))
-        nc.scalar.dma_start(out_word_rows[:, HALF:], out_words[:, HALF:].bitcast(I32))
+        nc.sync.dma_start(out_word_rows[:, HALF:], out_words[:, HALF:].bitcast(I32))
         for q in range(4):
-            eng = nc.scalar if q == 3 else nc.sync
+            eng = nc.scalar if q >= 2 else nc.sync
             eng.dma_start(out_2[0][q:16:4, :].bitcast(I32), out_scales[q:P:32, :].bitcast(I32))

@@ -119,9 +119,9 @@ def tile_picked_ptrjump_relu_po_kernel(
         )
 
         y_win = [keep.tile([P, 2 * S], F32, name="y_win%d" % t, align_bytes=64) for t in range(PACK)]
-        ring = keep.tile([P, 2 * PACK * PIECE], F32, name="ring", align_bytes=64)
+        ring = keep.tile([P, (2 * PACK + 2) * PIECE], F32, name="ring", align_bytes=64)
         y_dup = [keep.tile([P, S], F32, name="y_dup%d" % t, align_bytes=64)[:] for t in range(PACK - 1)]
-        y_dup.append(ring[:, PACK * PIECE :])
+        y_dup.append(ring[:, PACK * PIECE : 2 * PACK * PIECE])
         for part, (first, width, tag) in enumerate([(0, HALF, "y0_bank0"), (HALF, PIECE, "y0_bank1"), (HALF + PIECE, PIECE, "acc2")]):
             cols = slice(first, first + width)
             bank = psum.tile([P, width], F32, name="y0_part%d" % part, tag=tag)
@@ -165,7 +165,7 @@ def tile_picked_ptrjump_relu_po_kernel(
             return ap.rearrange("p t (c i) -> p c t i", i=4)
 
         def slots(c):
-            first = (c % 2) * PACK * PIECE
+            first = ((c % 2) * PACK + c // 2) * PIECE
             return ring[:, first : first + PACK * PIECE]
 
         def hop2(c, tiles):
@@ -178,13 +178,16 @@ def tile_picked_ptrjump_relu_po_kernel(
                     ALU.subtract,
                 )
 
-        zb3_room = ring[:, : 2 * PIECE].bitcast(BF16)
+        zb3_room = ring[:, PIECE : 3 * PIECE].bitcast(BF16)
 
         def rectify(c):
             src = planes(slots(c).rearrange("p (t n) -> p t n", t=PACK))
             if c < pieces - 1:
-                own = keep.tile([P, PACK * PIECE], BF16, name="zb%d" % c, tag="zq0" if c == 2 else "zb%d" % c, align_bytes=64)
-                zb[c] = own[:]
+                if c == 1:
+                    zb[c] = ring[:, 2 * PACK * PIECE :].bitcast(BF16)
+                else:
+                    own = keep.tile([P, PACK * PIECE], BF16, name="zb%d" % c, tag="zs0" if c == 2 else "zb0", align_bytes=64)
+                    zb[c] = own[:]
                 nc.scalar.activation(woven(zb[c]), src, ACT.Relu, scale=-1.0)
             else:
                 zb[c] = zb3_room
@@ -221,7 +224,7 @@ def tile_picked_ptrjump_relu_po_kernel(
                 nc.tensor.matmul_mx(
                     out=idle[:],
                     lhsT=codes[:].bitcast(FP8X4),
-                    lhsT_scale=scales[:],
+                    lhsT_scale=w2_s[:, :P],
                     rhs=xw[:].bitcast(FP8X4),
                     rhs_scale=xs[:],
                     start=True,
@@ -236,7 +239,8 @@ def tile_picked_ptrjump_relu_po_kernel(
             else:
                 for t in range(PACK):
                     nc.scalar.copy(of[c][:, t, :], acc[c][t])
-            nc.sync.dma_start(out_rows[:, :, cols], of[c][:])
+            queue = nc.scalar if c == last else nc.sync
+            queue.dma_start(out_rows[:, :, cols], of[c][:])
 
         def quantise_out(src, cols):
             nc.vector.quantize_mx(out=out_words[:, cols].bitcast(FP8X4), scales=out_scales[:, cols], in_=src)
@@ -249,10 +253,11 @@ def tile_picked_ptrjump_relu_po_kernel(
         rectify(1)
         layer2(0)
         store_values(0)
-        hop2(2, range(PACK))
-        rectify(2)
+        hop2(2, range(PACK - 1))
         layer2(1)
-        ob0 = keep.tile([P, PACK * PIECE], BF16, name="ob0", tag="zq1", align_bytes=64)[:]
+        hop2(2, [PACK - 1])
+        rectify(2)
+        ob0 = keep.tile([P, PACK * PIECE], BF16, name="ob0", tag="zs1", align_bytes=64)[:]
         ob1 = keep.tile([P, PACK * PIECE], BF16, name="ob1", align_bytes=64)
         ob23 = keep.tile([P, 2 * PACK * PIECE], BF16, name="ob23", align_bytes=64)
         store_values(1)

@@ -119,43 +119,68 @@ def tile_picked_ptrjump_relu_po_kernel(
         )
 
         y_win = [keep.tile([P, 2 * S], F32, name="y_win%d" % t, align_bytes=64) for t in range(PACK)]
-        ring = keep.tile([P, (2 * PACK + 2) * PIECE], F32, name="ring", align_bytes=64)
-        y_dup = [keep.tile([P, S], F32, name="y_dup%d" % t, align_bytes=64)[:] for t in range(PACK - 1)]
-        y_dup.append(ring[:, PACK * PIECE : 2 * PACK * PIECE])
-        for part, (first, width, tag) in enumerate([(0, HALF, "y0_bank0"), (HALF, PIECE, "y0_bank1"), (HALF + PIECE, PIECE, "acc2")]):
-            cols = slice(first, first + width)
-            bank = psum.tile([P, width], F32, name="y0_part%d" % part, tag=tag)
-            layer1(bank[:], 0, cols)
-            if part == 0:
-                nc.scalar.copy(y_win[0][:, cols], bank[:])
-            else:
-                nc.vector.tensor_copy(y_win[0][:, cols], bank[:])
-            nc.scalar.copy(y_dup[0][:, cols], bank[:])
-        quantise_w1(2, 2)
-        for t in range(1, PACK):
-            bank = psum.tile([P, S], F32, name="y_bank%d" % t)
-            layer1(bank[:], t, slice(0, S))
-            nc.scalar.copy(y_win[t][:, :S], bank[:])
-            nc.scalar.copy(y_dup[t], bank[:])
-
-        y_late = keep.tile([P, (PACK - 1) * PIECE], F32, name="y_late", tag="w1_q", align_bytes=64)
-        for t in range(PACK - 1):
-            nc.scalar.copy(y_late[:, t * PIECE : (t + 1) * PIECE], y_win[t][:, :PIECE])
-
-        e_win = [keep.tile([P, S], F32, name="e_win%d" % t, align_bytes=64) for t in range(PACK)]
+        p_win = [keep.tile([P, S], F32, name="p_win%d" % t, align_bytes=64) for t in range(PACK)]
         for h in range(2):
             cols = slice(h * HALF, (h + 1) * HALF)
-            half_list = par_t[:, h * HALF // 16 : (h + 1) * HALF // 16]
-            nc.vector.tensor_tensor(e_win[0][:, cols], y_win[0][:].indirect(half_list), y_dup[0][:, cols], ALU.subtract)
+            bank = psum.tile([P, HALF], F32, name="y0_bank%d" % h)
+            layer1(bank[:], 0, cols)
+            nc.scalar.copy(y_win[0][:, cols], bank[:])
+        quantise_w1(2, 2)
+        y_bank = {}
+        for t in range(1, PACK):
+            y_bank[t] = psum.tile([P, S], F32, name="y_bank%d" % t)
+            layer1(y_bank[t][:], t, slice(0, S))
+
+        def cols_of(c, count=1):
+            return slice(c * PIECE, (c + count) * PIECE)
+
+        def list_of(c, count=1):
+            return par_t[:, c * PIECE // 16 : (c + count) * PIECE // 16]
+
+        def parents(t):
+            nc.scalar.activation(p_win[t][:], y_win[t][:].indirect(par_t[:]), ACT.Copy)
+
+        sums = [keep.tile([P, S], F32, name="sum%d" % t, tag="w1_q" if t == 0 else "sum%d" % t, align_bytes=64) for t in range(PACK)]
+
+        def add_parents(t, c, count):
+            nc.vector.tensor_tensor(sums[t][:, cols_of(c, count)], y_win[t][:, cols_of(c, count)], p_win[t][:, cols_of(c, count)], ALU.add)
+
+        ring = keep.tile([P, (2 * PACK - 2) * HALF], F32, name="ring", align_bytes=64)
+
+        early = (PACK - 2) * HALF
+
+        def slot(t, c, count=1):
+            first = t * HALF + (early if c < 2 else 0) + c % 2 * PIECE
+            return ring[:, first : first + count * PIECE]
+
+        def piece(c):
+            first = early if c < 2 else 0
+            return ring[:, first : first + PACK * HALF].rearrange("p (t n) -> p t n", t=PACK)[:, :, cols_of(c % 2)]
+
+        def hop2(t, c, count=1):
+            nc.vector.tensor_tensor(slot(t, c, count), p_win[t][:].indirect(list_of(c, count)), sums[t][:, cols_of(c, count)], ALU.subtract)
+
+        grand = {}
+        grand_room = keep.tile([P, 3 * HALF], F32, name="grand_room", tag="y_win0", align_bytes=64)
+
+        def grandparents(t):
+            grand[t] = grand_room[:, t * HALF : (t + 1) * HALF] if t < PACK - 1 else sums[t][:, :HALF]
+            nc.scalar.activation(grand[t], p_win[t][:].indirect(list_of(2, 2)), ACT.Copy)
+
+        def take_grand(t, c=2, count=2):
+            nc.vector.tensor_tensor(slot(t, c, count), grand[t][:, cols_of(c - 2, count)], sums[t][:, cols_of(c, count)], ALU.subtract)
 
         out_words = keep.tile([P, S], U32, name="out_words", align_bytes=64)
         out_scales = keep.tile([P, S], U8, name="out_scales", align_bytes=64)
         out_rows = out_0.rearrange("(p t) c -> p t c", t=PACK)
         out_word_rows = out_1[0].rearrange("p n t -> p (n t)").bitcast(I32)
         pieces = S // PIECE
+        last = pieces - 1
         zb = {}
+        zq = {}
         acc = {}
         of = {}
+        ob = {}
         whole = {}
 
         def woven(ap):
@@ -164,49 +189,31 @@ def tile_picked_ptrjump_relu_po_kernel(
         def planes(ap):
             return ap.rearrange("p t (c i) -> p c t i", i=4)
 
-        def slots(c):
-            first = ((c % 2) * PACK + c // 2) * PIECE
-            return ring[:, first : first + PACK * PIECE]
-
-        def hop2(c, tiles):
-            cols = slice(c * PIECE, (c + 1) * PIECE)
-            for t in tiles:
-                nc.vector.tensor_tensor(
-                    slots(c)[:, t * PIECE : (t + 1) * PIECE],
-                    e_win[t][:].indirect(par_t[:, c * PIECE // 16 : (c + 1) * PIECE // 16]),
-                    y_late[:, t * PIECE : (t + 1) * PIECE] if c == 0 and t < PACK - 1 else y_win[t][:, cols],
-                    ALU.subtract,
-                )
-
-        zb3_room = ring[:, PIECE : 3 * PIECE].bitcast(BF16)
-
         def rectify(c):
-            src = planes(slots(c).rearrange("p (t n) -> p t n", t=PACK))
-            if c < pieces - 1:
-                if c == 1:
-                    zb[c] = ring[:, 2 * PACK * PIECE :].bitcast(BF16)
-                else:
-                    own = keep.tile([P, PACK * PIECE], BF16, name="zb%d" % c, tag="zs0" if c == 2 else "zb0", align_bytes=64)
-                    zb[c] = own[:]
-                nc.scalar.activation(woven(zb[c]), src, ACT.Relu, scale=-1.0)
+            src = planes(piece(c))
+            zb[c] = keep.tile([P, PACK * PIECE], BF16, name="zb%d" % c, align_bytes=64)
+            if c == 1:
+                nc.scalar.activation(woven(zb[c][:]), src, ACT.Relu, scale=-1.0)
             else:
-                zb[c] = zb3_room
-                nc.vector.tensor_scalar(woven(zb[c]), src, -1.0, 0.0, ALU.mult, ALU.max)
+                nc.vector.tensor_scalar(woven(zb[c][:]), src, -1.0, 0.0, ALU.mult, ALU.max)
 
-        last = pieces - 1
+        groups = {
+            0: [(0, 2, "acc0"), (2, 2, "acc1")],
+            1: [(0, 2, "acc2"), (2, 2, "y0_bank0")],
+            2: [(0, 2, "y0_bank1"), (2, 2, "y_bank1")],
+            3: [(0, 2, "y_bank2"), (2, 2, "y_bank3")],
+        }
 
         def layer2(c):
             codes = keep.tile([P, PIECE], U32, name="zq%d" % c, align_bytes=64)
             scales = keep.tile([P, PIECE], U8, name="zs%d" % c, align_bytes=64)
-            nc.vector.quantize_mx(out=codes[:].bitcast(FP8X4), scales=scales[:], in_=zb[c])
-            if c < last:
-                bank = psum.tile([P, PACK, PIECE], F32, name="acc%d" % c)
-                acc[c] = [bank[:, t, :] for t in range(PACK)]
-                whole[c] = bank
-            else:
-                tags = ["y0_bank0", "y0_bank1", "y_bank1", "y_bank2"]
-                banks = [psum.tile([P, PIECE], F32, name="last%d" % t, tag=tags[t]) for t in range(PACK)]
-                acc[c] = [bank[:] for bank in banks]
+            nc.vector.quantize_mx(out=codes[:].bitcast(FP8X4), scales=scales[:], in_=zb[c][:])
+            acc[c] = []
+            whole[c] = []
+            for first, count, tag in groups[c]:
+                bank = psum.tile([P, count, PIECE], F32, name="acc%d_%d" % (c, first), tag=tag)
+                acc[c].extend(bank[:, u, :] for u in range(count))
+                whole[c].append(bank)
             for t in range(PACK):
                 rows = slice(t * P, (t + 1) * P)
                 nc.tensor.matmul_mx(
@@ -219,64 +226,67 @@ def tile_picked_ptrjump_relu_po_kernel(
                     stop=True,
                 )
 
-            if c < 2:
-                idle = psum.tile([P, S], F32, name="idle%d" % c, tag="y_bank3")
-                nc.tensor.matmul_mx(
-                    out=idle[:],
-                    lhsT=codes[:].bitcast(FP8X4),
-                    lhsT_scale=w2_s[:, :P],
-                    rhs=xw[:].bitcast(FP8X4),
-                    rhs_scale=xs[:],
-                    start=True,
-                    stop=True,
-                )
-
         def store_values(c):
-            cols = slice(c * PIECE, (c + 1) * PIECE)
             of[c] = keep.tile([P, PACK, PIECE], F32, name="of%d" % c, align_bytes=64)
-            if c < last:
-                nc.scalar.copy(of[c][:], whole[c][:])
-            else:
-                for t in range(PACK):
-                    nc.scalar.copy(of[c][:, t, :], acc[c][t])
-            queue = nc.scalar if c == last else nc.sync
-            queue.dma_start(out_rows[:, :, cols], of[c][:])
+            for (first, count, tag), bank in zip(groups[c], whole[c]):
+                if c == last and first == 0:
+                    nc.vector.tensor_copy(of[c][:, first : first + count, :], bank[:])
+                else:
+                    nc.scalar.copy(of[c][:, first : first + count, :], bank[:])
+                if c < last:
+                    nc.sync.dma_start(out_rows[:, first : first + count, cols_of(c)], of[c][:, first : first + count, :])
+            if c == last:
+                nc.scalar.dma_start(out_rows[:, :, cols_of(c)], of[c][:])
 
-        def quantise_out(src, cols):
-            nc.vector.quantize_mx(out=out_words[:, cols].bitcast(FP8X4), scales=out_scales[:, cols], in_=src)
+        def round_out(c):
+            ob[c] = keep.tile([P, PACK * PIECE], BF16, name="ob%d" % c, tag="zs1" if c == 0 else "ob%d" % c, align_bytes=64)
+            if c == 0:
+                nc.scalar.activation(woven(ob[c][:]), planes(of[c][:]), ACT.Copy)
+            else:
+                nc.vector.tensor_copy(woven(ob[c][:]), planes(of[c][:]))
+
+        def quantise_out(c):
+            nc.vector.quantize_mx(out=out_words[:, cols_of(c)].bitcast(FP8X4), scales=out_scales[:, cols_of(c)], in_=ob[c][:])
 
         for t in range(1, PACK):
-            nc.vector.tensor_tensor(e_win[t][:], y_win[t][:].indirect(par_t[:]), y_dup[t], ALU.subtract)
-        hop2(0, range(PACK))
+            nc.vector.tensor_copy(y_win[t][:, :S], y_bank[t][:])
+        for t in range(PACK):
+            parents(t)
+            add_parents(t, 0, 2)
+            add_parents(t, 2, 2)
+            if t < PACK - 1:
+                hop2(t, 0, 2)
+        for t in range(PACK - 1):
+            grandparents(t)
+        hop2(3, 0)
+        hop2(3, 1)
         rectify(0)
-        hop2(1, range(PACK))
         rectify(1)
+        grandparents(3)
+        take_grand(0)
         layer2(0)
         store_values(0)
-        hop2(2, range(PACK - 1))
+        take_grand(1)
         layer2(1)
-        hop2(2, [PACK - 1])
-        rectify(2)
-        ob0 = keep.tile([P, PACK * PIECE], BF16, name="ob0", tag="zs1", align_bytes=64)[:]
-        ob1 = keep.tile([P, PACK * PIECE], BF16, name="ob1", align_bytes=64)
-        ob23 = keep.tile([P, 2 * PACK * PIECE], BF16, name="ob23", align_bytes=64)
         store_values(1)
-        nc.scalar.copy(ob0.rearrange("p (n t) -> p n t", t=PACK), whole[0][:].rearrange("p t n -> p n t"))
-        hop2(3, range(PACK))
+        round_out(0)
+        take_grand(2)
+        take_grand(3, 2, 1)
+        take_grand(3, 3, 1)
+        rectify(2)
+        rectify(3)
         layer2(2)
-        rectify(last)
         layer2(3)
-        nc.vector.tensor_copy(woven(ob1[:]), planes(of[1][:]))
-        quantise_out(ob0, slice(0, PIECE))
-        quantise_out(ob1[:], slice(PIECE, HALF))
-        nc.sync.dma_start(out_word_rows[:, :HALF], out_words[:, :HALF].bitcast(I32))
         store_values(2)
+        round_out(1)
+        quantise_out(0)
+        quantise_out(1)
         store_values(3)
-        for c in (2, 3):
-            nc.vector.tensor_copy(woven(ob23[:, (c - 2) * PACK * PIECE : (c - 1) * PACK * PIECE]), planes(of[c][:]))
-        for c in (2, 3):
-            quantise_out(ob23[:, (c - 2) * PACK * PIECE : (c - 1) * PACK * PIECE], slice(c * PIECE, (c + 1) * PIECE))
-        nc.sync.dma_start(out_word_rows[:, HALF:], out_words[:, HALF:].bitcast(I32))
+        round_out(2)
+        round_out(3)
+        quantise_out(2)
+        quantise_out(3)
+        nc.sync.dma_start(out_word_rows, out_words[:].bitcast(I32))
         for q in range(4):
             eng = nc.scalar if q >= 2 else nc.sync
             eng.dma_start(out_2[0][q:16:4, :].bitcast(I32), out_scales[q:P:32, :].bitcast(I32))

@@ -19,6 +19,12 @@ P = 128
 PACK = 4
 HALF = S // 2
 PIECE = 128
+PIECES = S // PIECE
+BANKS = 8
+FIRST_PAIR_SPLIT = 96
+SECOND_PAIR_SPLIT = 56
+ROWS_AT = slice(16, 32)
+CLEARED = ((0, 16), (32, 64), (64, P))
 
 
 def tile_picked_ptrjump_relu_po_kernel(
@@ -39,22 +45,28 @@ def tile_picked_ptrjump_relu_po_kernel(
 
         xs = keep.tile([P, S], U8, name="xs", align_bytes=64)
         w2_s = keep.tile([P, N], U8, name="w2_s", align_bytes=64)
-        nc.sync.dma_start(xs_table[16:32, :].bitcast(I32), x_scales[0].bitcast(I32))
-        for lo, hi in ((0, 16), (32, 64), (64, P)):
+        nc.sync.dma_start(xs_table[ROWS_AT, :].bitcast(I32), x_scales[0].bitcast(I32))
+        for lo, hi in CLEARED:
             nc.vector.memset(xs_table[lo:hi, :].bitcast(I32), 0)
         nc.gpsimd.memset(xs[:].bitcast(I32), 0)
-        for lo, hi in ((0, 16), (32, 64), (64, P)):
+        for lo, hi in CLEARED:
             nc.gpsimd.memset(w2s_raw[lo:hi, :].bitcast(I32), 0)
         nc.gpsimd.memset(w2_s[:].bitcast(I32), 0)
         nc.sync.dma_start(offs_t[:], offs)
         nc.sync.dma_start(x_table[:].bitcast(I32), x_words[0].rearrange("p n t -> p (n t)").bitcast(I32))
-        nc.sync.dma_start(w2s_raw[16:32, :].bitcast(I32), w2_scales[0].bitcast(I32))
+        nc.sync.dma_start(w2s_raw[ROWS_AT, :].bitcast(I32), w2_scales[0].bitcast(I32))
         nc.sync.dma_start(w1_raw[:], w1.rearrange("(p j) c -> p j c", j=PACK))
         nc.sync.dma_start(par_t[:], par)
 
         def move_rows(plane, spread):
             for r in range(4):
                 nc.sync.dma_start(plane[r:P:32, :].bitcast(I32), spread[16 + r : 32 : 4, :].bitcast(I32))
+
+        def dealt(ap):
+            return ap.rearrange("p (t m) -> p m t", t=PACK)
+
+        def undealt(ap):
+            return ap.rearrange("p (m t) -> p m t", t=PACK)
 
         xs_spread = keep.tile([P, S], U8, name="xs_spread", align_bytes=64)
         nc.vector.tensor_copy(xs_spread[:], xs_table[:].indirect(offs_t[:]))
@@ -66,9 +78,7 @@ def tile_picked_ptrjump_relu_po_kernel(
         nc.vector.tensor_copy(xw[:], x_table[:].indirect(offs_t[:]))
 
         w2s_spread = keep.tile([P, N], U8, name="w2s_spread", align_bytes=64)
-        nc.vector.tensor_copy(
-            w2s_spread[:].rearrange("p (t m) -> p m t", t=PACK), w2s_raw[:].rearrange("p (m t) -> p m t", t=PACK)
-        )
+        nc.vector.tensor_copy(dealt(w2s_spread[:]), undealt(w2s_raw[:]))
         move_rows(w2_s, w2s_spread)
 
         w1_src = w1_raw[:].rearrange("p j (m t) -> p m j t", t=PACK)
@@ -77,59 +87,29 @@ def tile_picked_ptrjump_relu_po_kernel(
         w1_b = [keep.tile([P, 2 * H], BF16, name="w1_b%d" % u, align_bytes=64) for u in range(2)]
         w1_dst = [w1_b[u][:].rearrange("p (t m j) -> p m j t", t=2, j=PACK) for u in range(2)]
 
-        def round_w1(engine, u, lo, hi):
-            src = w1_src[:, lo:hi, :, 2 * u : 2 * u + 2]
+        def round_w1(engine, pair, lo, hi):
+            src = w1_src[:, lo:hi, :, 2 * pair : 2 * pair + 2]
             if engine == "scalar":
-                nc.scalar.activation(w1_dst[u][:, lo:hi], src, ACT.Copy)
+                nc.scalar.activation(w1_dst[pair][:, lo:hi], src, ACT.Copy)
             else:
-                nc.vector.tensor_copy(w1_dst[u][:, lo:hi], src)
+                nc.vector.tensor_copy(w1_dst[pair][:, lo:hi], src)
 
-        round_w1("scalar", 0, 96, P)
-        round_w1("vector", 0, 0, 64)
-        round_w1("vector", 0, 64, 96)
-        round_w1("scalar", 1, 56, P)
+        def quantise_w1(lo, hi):
+            pair = lo // (2 * P)
+            src = w1_b[pair][:, PACK * (lo - 2 * P * pair) : PACK * (hi - 2 * P * pair)]
+            nc.vector.quantize_mx(out=w1_q[:, lo:hi].bitcast(FP8X4), scales=w1_s[:, lo:hi], in_=src)
 
-        def quantise_w1(first, count):
-            cols = slice(first * P, (first + count) * P)
-            src = w1_b[first // 2][:, (first % 2) * H : (first % 2 + count) * H]
-            nc.vector.quantize_mx(out=w1_q[:, cols].bitcast(FP8X4), scales=w1_s[:, cols], in_=src)
-
-        for lo in (0, 64):
-            nc.vector.quantize_mx(
-                out=w1_q[:, lo : lo + 64].bitcast(FP8X4), scales=w1_s[:, lo : lo + 64], in_=w1_b[0][:, 4 * lo : 4 * lo + 256]
-            )
-        round_w1("vector", 1, 0, 56)
-        quantise_w1(1, 1)
-
-        def layer1(bank, t, cols):
-            rows = slice(t * P, (t + 1) * P)
-            nc.tensor.matmul_mx(
-                out=bank,
-                lhsT=w1_q[:, rows].bitcast(FP8X4),
-                lhsT_scale=w1_s[:, rows],
-                rhs=xw[:, cols].bitcast(FP8X4),
-                rhs_scale=xs[:, cols],
-                start=True,
-                stop=True,
-            )
+        round_w1("scalar", 0, FIRST_PAIR_SPLIT, P)
+        round_w1("vector", 0, 0, P // 2)
+        round_w1("vector", 0, P // 2, FIRST_PAIR_SPLIT)
+        round_w1("scalar", 1, SECOND_PAIR_SPLIT, P)
+        quantise_w1(0, P // 2)
+        quantise_w1(P // 2, P)
+        round_w1("vector", 1, 0, SECOND_PAIR_SPLIT)
+        quantise_w1(P, 2 * P)
 
         w2_q = keep.tile([P, N], I32, name="w2_q", tag="x_table", align_bytes=64)
-        nc.vector.tensor_copy(
-            w2_q[:].rearrange("p (t m) -> p m t", t=PACK), w2_raw[:].rearrange("p (m t) -> p m t", t=PACK)
-        )
-
-        y_win = [keep.tile([P, 2 * S], F32, name="y_win%d" % t, align_bytes=64) for t in range(PACK)]
-        p_win = [keep.tile([P, S], F32, name="p_win%d" % t, align_bytes=64) for t in range(PACK)]
-        for h in range(2):
-            cols = slice(h * HALF, (h + 1) * HALF)
-            bank = psum.tile([P, HALF], F32, name="y0_bank%d" % h)
-            layer1(bank[:], 0, cols)
-            nc.scalar.copy(y_win[0][:, cols], bank[:])
-        quantise_w1(2, 2)
-        y_bank = {}
-        for t in range(1, PACK):
-            y_bank[t] = psum.tile([P, S], F32, name="y_bank%d" % t)
-            layer1(y_bank[t][:], t, slice(0, S))
+        nc.vector.tensor_copy(dealt(w2_q[:]), undealt(w2_raw[:]))
 
         def cols_of(c, count=1):
             return slice(c * PIECE, (c + count) * PIECE)
@@ -137,87 +117,116 @@ def tile_picked_ptrjump_relu_po_kernel(
         def list_of(c, count=1):
             return par_t[:, c * PIECE // 16 : (c + count) * PIECE // 16]
 
+        def copy_out(engine, dst, bank):
+            if engine == "scalar":
+                nc.scalar.copy(dst, bank)
+            else:
+                nc.vector.tensor_copy(dst, bank)
+
+        y_win = [keep.tile([P, 2 * S], F32, name="y_win%d" % t, align_bytes=64) for t in range(PACK)]
+        p_win = [keep.tile([P, S], F32, name="p_win%d" % t, align_bytes=64) for t in range(PACK)]
+
+        def layer1(engine, t, cols, number):
+            bank = psum.tile([P, cols.stop - cols.start], F32, name="y%d_%d" % (t, cols.start), tag="bank%d" % number)
+            rows = slice(t * P, (t + 1) * P)
+            nc.tensor.matmul_mx(
+                out=bank[:],
+                lhsT=w1_q[:, rows].bitcast(FP8X4),
+                lhsT_scale=w1_s[:, rows],
+                rhs=xw[:, cols].bitcast(FP8X4),
+                rhs_scale=xs[:, cols],
+                start=True,
+                stop=True,
+            )
+            copy_out(engine, y_win[t][:, cols], bank[:])
+
+        for c in range(PIECES):
+            layer1("scalar", 0, cols_of(c), c)
+        quantise_w1(2 * P, PACK * P)
+        for t in range(1, PACK):
+            for h in range(2):
+                engine = "scalar" if (t, h) == (1, 0) else "vector"
+                layer1(engine, t, cols_of(2 * h, 2), (PIECES + 2 * (t - 1) + h) % BANKS)
+
         def parents(t):
             nc.scalar.activation(p_win[t][:], y_win[t][:].indirect(par_t[:]), ACT.Copy)
 
-        sums = [keep.tile([P, S], F32, name="sum%d" % t, tag="w1_q" if t == 0 else "sum%d" % t, align_bytes=64) for t in range(PACK)]
+        sums = [
+            keep.tile([P, S], F32, name="sum%d" % t, tag="w1_q" if t == 0 else "sum%d" % t, align_bytes=64)
+            for t in range(PACK)
+        ]
 
         def add_parents(t, c, count):
-            nc.vector.tensor_tensor(sums[t][:, cols_of(c, count)], y_win[t][:, cols_of(c, count)], p_win[t][:, cols_of(c, count)], ALU.add)
-
-        ring = keep.tile([P, (2 * PACK - 2) * HALF], F32, name="ring", align_bytes=64)
+            cols = cols_of(c, count)
+            nc.vector.tensor_tensor(sums[t][:, cols], y_win[t][:, cols], p_win[t][:, cols], ALU.add)
 
         early = (PACK - 2) * HALF
+        minus_z = keep.tile([P, early + PACK * HALF], F32, name="minus_z", align_bytes=64)
 
-        def slot(t, c, count=1):
+        def part_of(t, c, count):
             first = t * HALF + (early if c < 2 else 0) + c % 2 * PIECE
-            return ring[:, first : first + count * PIECE]
+            return minus_z[:, first : first + count * PIECE]
 
-        def piece(c):
+        def piece_of(c):
             first = early if c < 2 else 0
-            return ring[:, first : first + PACK * HALF].rearrange("p (t n) -> p t n", t=PACK)[:, :, cols_of(c % 2)]
+            return minus_z[:, first : first + PACK * HALF].rearrange("p (t n) -> p t n", t=PACK)[:, :, cols_of(c % 2)]
 
-        def hop2(t, c, count=1):
-            nc.vector.tensor_tensor(slot(t, c, count), p_win[t][:].indirect(list_of(c, count)), sums[t][:, cols_of(c, count)], ALU.subtract)
+        def fused_grandparents(t, c, count):
+            window = p_win[t][:].indirect(list_of(c, count))
+            nc.vector.tensor_tensor(part_of(t, c, count), window, sums[t][:, cols_of(c, count)], ALU.subtract)
 
-        grand = {}
-        grand_room = keep.tile([P, 3 * HALF], F32, name="grand_room", tag="y_win0", align_bytes=64)
+        grand_room = keep.tile([P, (PACK - 1) * HALF], F32, name="grand_room", tag="y_win0", align_bytes=64)
+        grand = [grand_room[:, t * HALF : (t + 1) * HALF] for t in range(PACK - 1)] + [sums[PACK - 1][:, :HALF]]
 
-        def grandparents(t):
-            grand[t] = grand_room[:, t * HALF : (t + 1) * HALF] if t < PACK - 1 else sums[t][:, :HALF]
+        def late_grandparents(t):
             nc.scalar.activation(grand[t], p_win[t][:].indirect(list_of(2, 2)), ACT.Copy)
 
-        def take_grand(t, c=2, count=2):
-            nc.vector.tensor_tensor(slot(t, c, count), grand[t][:, cols_of(c - 2, count)], sums[t][:, cols_of(c, count)], ALU.subtract)
+        def subtract_sums(t, c, count):
+            q = grand[t][:, cols_of(c - 2, count)]
+            nc.vector.tensor_tensor(part_of(t, c, count), q, sums[t][:, cols_of(c, count)], ALU.subtract)
 
         out_words = keep.tile([P, S], U32, name="out_words", align_bytes=64)
         out_scales = keep.tile([P, S], U8, name="out_scales", align_bytes=64)
         out_rows = out_0.rearrange("(p t) c -> p t c", t=PACK)
-        out_word_rows = out_1[0].rearrange("p n t -> p (n t)").bitcast(I32)
-        pieces = S // PIECE
-        last = pieces - 1
-        zb = {}
-        zq = {}
-        acc = {}
-        of = {}
-        ob = {}
-        whole = {}
+        z_rounded = {}
+        z_packed = {}
+        values = {}
+        values_rounded = {}
+        banks = {}
 
         def woven(ap):
             return ap.rearrange("p (c i t) -> p c t i", i=4, t=PACK)
 
-        def planes(ap):
+        def row_tiles(ap):
             return ap.rearrange("p t (c i) -> p c t i", i=4)
 
-        def rectify(c):
-            src = planes(piece(c))
-            zb[c] = keep.tile([P, PACK * PIECE], BF16, name="zb%d" % c, align_bytes=64)
-            if c == 1:
-                nc.scalar.activation(woven(zb[c][:]), src, ACT.Relu, scale=-1.0)
+        def rectify(engine, c):
+            z_rounded[c] = keep.tile([P, PACK * PIECE], BF16, name="zb%d" % c, align_bytes=64)
+            if engine == "scalar":
+                nc.scalar.activation(woven(z_rounded[c][:]), row_tiles(piece_of(c)), ACT.Relu, scale=-1.0)
             else:
-                nc.vector.tensor_scalar(woven(zb[c][:]), src, -1.0, 0.0, ALU.mult, ALU.max)
+                nc.vector.tensor_scalar(woven(z_rounded[c][:]), row_tiles(piece_of(c)), -1.0, 0.0, ALU.mult, ALU.max)
 
-        groups = {
-            0: [(0, 2, "acc0"), (2, 2, "acc1")],
-            1: [(0, 2, "acc2"), (2, 2, "y0_bank0")],
-            2: [(0, 2, "y0_bank1"), (2, 2, "y_bank1")],
-            3: [(0, 2, "y_bank2"), (2, 2, "y_bank3")],
-        }
+        late_values = keep.tile([P, PACK, HALF], F32, name="late_values", align_bytes=64)
 
-        def layer2(c):
+        def quantise_z(c):
             codes = keep.tile([P, PIECE], U32, name="zq%d" % c, align_bytes=64)
             scales = keep.tile([P, PIECE], U8, name="zs%d" % c, align_bytes=64)
-            nc.vector.quantize_mx(out=codes[:].bitcast(FP8X4), scales=scales[:], in_=zb[c][:])
-            acc[c] = []
-            whole[c] = []
-            for first, count, tag in groups[c]:
-                bank = psum.tile([P, count, PIECE], F32, name="acc%d_%d" % (c, first), tag=tag)
-                acc[c].extend(bank[:, u, :] for u in range(count))
-                whole[c].append(bank)
-            for t in range(PACK):
-                rows = slice(t * P, (t + 1) * P)
+            nc.vector.quantize_mx(out=codes[:].bitcast(FP8X4), scales=scales[:], in_=z_rounded[c][:])
+            z_packed[c] = (codes, scales)
+            if c < 2:
+                values[c] = keep.tile([P, PACK, PIECE], F32, name="values%d" % c, align_bytes=64)[:]
+            else:
+                values[c] = late_values[:, :, cols_of(c - 2)]
+
+        def layer2(c, first, count, number):
+            bank = psum.tile([P, count, PIECE], F32, name="acc%d_%d" % (c, first), tag="bank%d" % number)
+            banks[c, first] = bank
+            codes, scales = z_packed[c]
+            for u in range(count):
+                rows = slice((first + u) * P, (first + u + 1) * P)
                 nc.tensor.matmul_mx(
-                    out=acc[c][t],
+                    out=bank[:, u, :],
                     lhsT=w2_q[:, rows].bitcast(FP8X4),
                     lhsT_scale=w2_s[:, rows],
                     rhs=codes[:].bitcast(FP8X4),
@@ -226,67 +235,83 @@ def tile_picked_ptrjump_relu_po_kernel(
                     stop=True,
                 )
 
-        def store_values(c):
-            of[c] = keep.tile([P, PACK, PIECE], F32, name="of%d" % c, align_bytes=64)
-            for (first, count, tag), bank in zip(groups[c], whole[c]):
-                if c == last and first == 0:
-                    nc.vector.tensor_copy(of[c][:, first : first + count, :], bank[:])
-                else:
-                    nc.scalar.copy(of[c][:, first : first + count, :], bank[:])
-                if c < last:
-                    nc.sync.dma_start(out_rows[:, first : first + count, cols_of(c)], of[c][:, first : first + count, :])
-            if c == last:
-                nc.scalar.dma_start(out_rows[:, :, cols_of(c)], of[c][:])
+        def values_out(engine, c, first, count):
+            copy_out(engine, values[c][:, first : first + count, :], banks[c, first][:])
 
-        def round_out(c):
-            ob[c] = keep.tile([P, PACK * PIECE], BF16, name="ob%d" % c, tag="zs1" if c == 0 else "ob%d" % c, align_bytes=64)
-            if c == 0:
-                nc.scalar.activation(woven(ob[c][:]), planes(of[c][:]), ACT.Copy)
+        def store_early(c, first, count):
+            nc.sync.dma_start(out_rows[:, first : first + count, cols_of(c)], values[c][:, first : first + count, :])
+
+        def store_late(queue, first, count):
+            queue.dma_start(out_rows[:, first : first + count, HALF:], late_values[:, first : first + count, :])
+
+        def round_values(engine, c):
+            tag = "zs1" if c == 0 else "ob%d" % c
+            values_rounded[c] = keep.tile([P, PACK * PIECE], BF16, name="ob%d" % c, tag=tag, align_bytes=64)
+            if engine == "scalar":
+                nc.scalar.activation(woven(values_rounded[c][:]), row_tiles(values[c]), ACT.Copy)
             else:
-                nc.vector.tensor_copy(woven(ob[c][:]), planes(of[c][:]))
+                nc.vector.tensor_copy(woven(values_rounded[c][:]), row_tiles(values[c]))
 
-        def quantise_out(c):
-            nc.vector.quantize_mx(out=out_words[:, cols_of(c)].bitcast(FP8X4), scales=out_scales[:, cols_of(c)], in_=ob[c][:])
+        def quantise_values(c):
+            cols = cols_of(c)
+            nc.vector.quantize_mx(out=out_words[:, cols].bitcast(FP8X4), scales=out_scales[:, cols], in_=values_rounded[c][:])
 
-        for t in range(1, PACK):
-            nc.vector.tensor_copy(y_win[t][:, :S], y_bank[t][:])
+        last = PACK - 1
         for t in range(PACK):
             parents(t)
             add_parents(t, 0, 2)
             add_parents(t, 2, 2)
-            if t < PACK - 1:
-                hop2(t, 0, 2)
-        for t in range(PACK - 1):
-            grandparents(t)
-        hop2(3, 0)
-        hop2(3, 1)
-        rectify(0)
-        rectify(1)
-        grandparents(3)
-        take_grand(0)
-        layer2(0)
-        store_values(0)
-        take_grand(1)
-        layer2(1)
-        store_values(1)
-        round_out(0)
-        take_grand(2)
-        take_grand(3, 2, 1)
-        take_grand(3, 3, 1)
-        rectify(2)
-        rectify(3)
-        layer2(2)
-        layer2(3)
-        store_values(2)
-        round_out(1)
-        quantise_out(0)
-        quantise_out(1)
-        store_values(3)
-        round_out(2)
-        round_out(3)
-        quantise_out(2)
-        quantise_out(3)
-        nc.sync.dma_start(out_word_rows, out_words[:].bitcast(I32))
-        for q in range(4):
-            eng = nc.scalar if q >= 2 else nc.sync
-            eng.dma_start(out_2[0][q:16:4, :].bitcast(I32), out_scales[q:P:32, :].bitcast(I32))
+            if t < last:
+                fused_grandparents(t, 0, 2)
+        for t in range(last):
+            late_grandparents(t)
+        fused_grandparents(last, 0, 1)
+        fused_grandparents(last, 1, 1)
+
+        rectify("vector", 0)
+        rectify("scalar", 1)
+        late_grandparents(last)
+        subtract_sums(0, 2, 2)
+        quantise_z(0)
+        for h in range(2):
+            layer2(0, 2 * h, 2, h)
+            values_out("scalar", 0, 2 * h, 2)
+            store_early(0, 2 * h, 2)
+        subtract_sums(1, 2, 2)
+        quantise_z(1)
+        for h in range(2):
+            layer2(1, 2 * h, 2, 2 + h)
+            values_out("scalar", 1, 2 * h, 2)
+        store_early(1, 0, PACK)
+        round_values("scalar", 0)
+
+        subtract_sums(2, 2, 2)
+        subtract_sums(last, 2, 1)
+        subtract_sums(last, 3, 1)
+        rectify("vector", 2)
+        rectify("vector", 3)
+        quantise_z(2)
+        quantise_z(3)
+        layer2(2, 0, 2, 4)
+        layer2(3, 0, 1, 5)
+        layer2(3, 1, 1, 6)
+        layer2(2, 2, 2, 3)
+        layer2(3, 2, 2, 7)
+        round_values("vector", 1)
+        values_out("scalar", 2, 0, 2)
+        for t in range(2):
+            values_out("scalar", 3, t, 1)
+            store_late(nc.sync, t, 1)
+        quantise_values(1)
+        values_out("vector", 2, 2, 2)
+        values_out("scalar", 3, 2, 2)
+        store_late(nc.scalar, 2, 2)
+        quantise_values(0)
+        round_values("vector", 2)
+        round_values("vector", 3)
+        quantise_values(2)
+        quantise_values(3)
+
+        nc.sync.dma_start(out_1[0].rearrange("p n t -> p (n t)").bitcast(I32), out_words[:].bitcast(I32))
+        for r in range(4):
+            nc.scalar.dma_start(out_2[0][r:16:4, :].bitcast(I32), out_scales[r:P:32, :].bitcast(I32))

@@ -1,6 +1,7 @@
 from contextlib import ExitStack
 
 import concourse.mybir as mybir
+from concourse.masks import make_identity
 
 K, T, S, H, N = 512, 2048, 512, 512, 512
 FLOPS = 2 * K * H * S + 2 * H * N * S
@@ -52,6 +53,8 @@ def tile_picked_ptrjump_relu_po_kernel(
         for lo, hi in CLEARED:
             nc.gpsimd.memset(w2s_raw[lo:hi, :].bitcast(I32), 0)
         nc.gpsimd.memset(w2_s[:].bitcast(I32), 0)
+        identity = keep.tile([P, P], F32, name="identity", align_bytes=64)
+        make_identity(nc, identity[:])
         nc.sync.dma_start(offs_t[:], offs)
         nc.sync.dma_start(x_table[:].bitcast(I32), x_words[0].rearrange("p n t -> p (n t)").bitcast(I32))
         nc.sync.dma_start(w2s_raw[ROWS_AT, :].bitcast(I32), w2_scales[0].bitcast(I32))
@@ -148,51 +151,70 @@ def tile_picked_ptrjump_relu_po_kernel(
                 engine = "scalar" if (t, h) == (1, 0) else "vector"
                 layer1(engine, t, cols_of(2 * h, 2), (PIECES + 2 * (t - 1) + h) % BANKS)
 
+        TURNED = (2, 3)
+        last = PACK - 1
+
         def parents(t):
             nc.scalar.activation(p_win[t][:], y_win[t][:].indirect(par_t[:]), ACT.Copy)
 
         sums = [
-            keep.tile([P, S], F32, name="sum%d" % t, tag="w1_q" if t == 0 else "sum%d" % t, align_bytes=64)
+            keep.tile([P, HALF], F32, name="sum%d" % t, tag="w1_q" if t == 0 else "sum%d" % t, align_bytes=64)
             for t in range(PACK)
         ]
 
-        def add_parents(t, c, count):
-            cols = cols_of(c, count)
-            nc.vector.tensor_tensor(sums[t][:, cols], y_win[t][:, cols], p_win[t][:, cols], ALU.add)
+        def add_parents(t):
+            nc.vector.tensor_tensor(sums[t][:], y_win[t][:, :HALF], p_win[t][:, :HALF], ALU.add)
 
-        early = (PACK - 2) * HALF
-        minus_z = keep.tile([P, early + PACK * HALF], F32, name="minus_z", align_bytes=64)
-
-        def part_of(t, c, count):
-            first = t * HALF + (early if c < 2 else 0) + c % 2 * PIECE
-            return minus_z[:, first : first + count * PIECE]
-
-        def piece_of(c):
-            first = early if c < 2 else 0
-            return minus_z[:, first : first + PACK * HALF].rearrange("p (t n) -> p t n", t=PACK)[:, :, cols_of(c % 2)]
+        minus_room = keep.tile([P, PACK * HALF], F32, name="minus_room", align_bytes=64)
+        minus_rows = minus_room[:].rearrange("p (t n) -> p t n", t=PACK)
+        minus_z = [minus_rows[:, :, cols_of(c)] for c in range(2)]
 
         def fused_grandparents(t, c, count):
             window = p_win[t][:].indirect(list_of(c, count))
-            nc.vector.tensor_tensor(part_of(t, c, count), window, sums[t][:, cols_of(c, count)], ALU.subtract)
+            nc.vector.tensor_tensor(minus_rows[:, t, cols_of(c, count)], window, sums[t][:, cols_of(c, count)], ALU.subtract)
 
-        grand_room = keep.tile([P, (PACK - 1) * HALF], F32, name="grand_room", tag="y_win0", align_bytes=64)
-        grand = [grand_room[:, t * HALF : (t + 1) * HALF] for t in range(PACK - 1)] + [sums[PACK - 1][:, :HALF]]
+        minus_q = [keep.tile([P, HALF], F32, name="minus_q%d" % t, align_bytes=64) for t in range(PACK)]
 
-        def late_grandparents(t):
-            nc.scalar.activation(grand[t], p_win[t][:].indirect(list_of(2, 2)), ACT.Copy)
+        def vector_grandparents(t, count):
+            window = p_win[t][:].indirect(list_of(TURNED[0], count))
+            nc.vector.tensor_scalar(minus_q[t][:, cols_of(0, count)], window, -1.0, 0.0, ALU.mult, ALU.add)
 
-        def subtract_sums(t, c, count):
-            q = grand[t][:, cols_of(c - 2, count)]
-            nc.vector.tensor_tensor(part_of(t, c, count), q, sums[t][:, cols_of(c, count)], ALU.subtract)
+        def scalar_grandparents(t, c):
+            window = p_win[t][:].indirect(list_of(c))
+            nc.scalar.activation(minus_q[t][:, cols_of(c - TURNED[0])], window, ACT.Copy, scale=-1.0)
+
+        low = psum.tile([P, 2, 2, P], F32, name="low", tag="bank1")
+        high = {c: psum.tile([P, 2, P], F32, name="high%d" % c, tag="bank%d" % (1 + c)) for c in TURNED}
+        pairs = {c: psum.tile([P, 2, PIECE], F32, name="pairs%d" % c, tag="bank%d" % (3 + c)) for c in TURNED}
+
+        def turn(n, t, c):
+            out = low[:, c - TURNED[0], t, :] if t < 2 else high[c][:, t - 2, :]
+            source = (y_win[t][:, cols_of(c)], p_win[t][:, cols_of(c)], minus_q[t][:, cols_of(c - TURNED[0])])[n]
+            opens = n == 0 and (t == 2 or (t, c) == (0, TURNED[0]))
+            closes = n == 2 and (t == last or (t, c) == (1, TURNED[1]))
+            nc.tensor.matmul(out, source, identity[:], start=opens, stop=closes, is_transpose=True)
+
+        seen = {}
+
+        def rectify_turned(u, c):
+            src = low[:, c - TURNED[0]] if u == 0 else high[c][:]
+            turned = keep.tile([P, 2 * P], BF16, name="turned%d_%d" % (u, c), align_bytes=64)
+            nc.scalar.activation(
+                turned[:].rearrange("p (r e) -> p r e", e=2), src.rearrange("p e r -> p r e"), ACT.Relu
+            )
+            seen[u, c] = turned
+            nc.tensor.transpose(pairs[c][:, u, :], turned[:].bitcast(F32), identity[:])
 
         out_words = keep.tile([P, S], U32, name="out_words", align_bytes=64)
         out_scales = keep.tile([P, S], U8, name="out_scales", align_bytes=64)
         out_rows = out_0.rearrange("(p t) c -> p t c", t=PACK)
-        z_rounded = {}
+        words_rows = out_1[0].rearrange("p n t -> p (n t)").bitcast(I32)
+        z_rounded = [keep.tile([P, PACK * PIECE], BF16, name="zb%d" % c, align_bytes=64) for c in range(PIECES)]
+        late_values = keep.tile([P, PACK, HALF], F32, name="late_values", align_bytes=64)
+        values = [keep.tile([P, PACK, PIECE], F32, name="values%d" % c, align_bytes=64)[:] for c in range(2)]
+        values = values + [late_values[:, :, cols_of(c)] for c in range(2)]
         z_packed = {}
-        values = {}
         values_rounded = {}
-        banks = {}
 
         def woven(ap):
             return ap.rearrange("p (c i t) -> p c t i", i=4, t=PACK)
@@ -200,29 +222,26 @@ def tile_picked_ptrjump_relu_po_kernel(
         def row_tiles(ap):
             return ap.rearrange("p t (c i) -> p c t i", i=4)
 
+        def join_pairs(engine, c):
+            dst = z_rounded[c][:].bitcast(F32).rearrange("p (n u) -> p n u", u=2)
+            copy_out(engine, dst, pairs[c][:].rearrange("p u n -> p n u"))
+
         def rectify(engine, c):
-            z_rounded[c] = keep.tile([P, PACK * PIECE], BF16, name="zb%d" % c, align_bytes=64)
             if engine == "scalar":
-                nc.scalar.activation(woven(z_rounded[c][:]), row_tiles(piece_of(c)), ACT.Relu, scale=-1.0)
+                nc.scalar.activation(woven(z_rounded[c][:]), row_tiles(minus_z[c]), ACT.Relu, scale=-1.0)
             else:
-                nc.vector.tensor_scalar(woven(z_rounded[c][:]), row_tiles(piece_of(c)), -1.0, 0.0, ALU.mult, ALU.max)
+                nc.vector.tensor_scalar(woven(z_rounded[c][:]), row_tiles(minus_z[c]), -1.0, 0.0, ALU.mult, ALU.max)
 
-        late_values = keep.tile([P, PACK, HALF], F32, name="late_values", align_bytes=64)
-
-        def quantise_z(c):
+        def quantise_z(c, scales=None):
             codes = keep.tile([P, PIECE], U32, name="zq%d" % c, align_bytes=64)
-            scales = keep.tile([P, PIECE], U8, name="zs%d" % c, align_bytes=64)
-            nc.vector.quantize_mx(out=codes[:].bitcast(FP8X4), scales=scales[:], in_=z_rounded[c][:])
+            if scales is None:
+                scales = keep.tile([P, PIECE], U8, name="zs%d" % c, align_bytes=64)[:]
+            nc.vector.quantize_mx(out=codes[:].bitcast(FP8X4), scales=scales, in_=z_rounded[c][:])
             z_packed[c] = (codes, scales)
-            if c < 2:
-                values[c] = keep.tile([P, PACK, PIECE], F32, name="values%d" % c, align_bytes=64)[:]
-            else:
-                values[c] = late_values[:, :, cols_of(c - 2)]
 
-        def layer2(c, first, count, number):
-            bank = psum.tile([P, count, PIECE], F32, name="acc%d_%d" % (c, first), tag="bank%d" % number)
-            banks[c, first] = bank
+        def layer2(c, first, count, number, engine, step=PACK):
             codes, scales = z_packed[c]
+            bank = psum.tile([P, count, PIECE], F32, name="acc%d_%d" % (c, first), tag="bank%d" % number)
             for u in range(count):
                 rows = slice((first + u) * P, (first + u + 1) * P)
                 nc.tensor.matmul_mx(
@@ -230,22 +249,22 @@ def tile_picked_ptrjump_relu_po_kernel(
                     lhsT=w2_q[:, rows].bitcast(FP8X4),
                     lhsT_scale=w2_s[:, rows],
                     rhs=codes[:].bitcast(FP8X4),
-                    rhs_scale=scales[:],
+                    rhs_scale=scales,
                     start=True,
                     stop=True,
                 )
+            for u in range(0, count, step):
+                width = min(step, count)
+                copy_out(engine, values[c][:, first + u : first + u + width, :], bank[:, u : u + width, :])
 
-        def values_out(engine, c, first, count):
-            copy_out(engine, values[c][:, first : first + count, :], banks[c, first][:])
-
-        def store_early(c, first, count):
-            nc.sync.dma_start(out_rows[:, first : first + count, cols_of(c)], values[c][:, first : first + count, :])
+        def store_values(queue, c, first, count):
+            queue.dma_start(out_rows[:, first : first + count, cols_of(c)], values[c][:, first : first + count, :])
 
         def store_late(queue, first, count):
             queue.dma_start(out_rows[:, first : first + count, HALF:], late_values[:, first : first + count, :])
 
         def round_values(engine, c):
-            tag = "zs1" if c == 0 else "ob%d" % c
+            tag = "zs3" if c == 1 else "ob%d" % c
             values_rounded[c] = keep.tile([P, PACK * PIECE], BF16, name="ob%d" % c, tag=tag, align_bytes=64)
             if engine == "scalar":
                 nc.scalar.activation(woven(values_rounded[c][:]), row_tiles(values[c]), ACT.Copy)
@@ -256,62 +275,69 @@ def tile_picked_ptrjump_relu_po_kernel(
             cols = cols_of(c)
             nc.vector.quantize_mx(out=out_words[:, cols].bitcast(FP8X4), scales=out_scales[:, cols], in_=values_rounded[c][:])
 
-        last = PACK - 1
         for t in range(PACK):
+            for c in TURNED:
+                turn(0, t, c)
+        for t in range(2):
             parents(t)
-            add_parents(t, 0, 2)
-            add_parents(t, 2, 2)
-            if t < last:
-                fused_grandparents(t, 0, 2)
-        for t in range(last):
-            late_grandparents(t)
+            add_parents(t)
+            vector_grandparents(t, 2)
+            for n in (1, 2):
+                for c in TURNED:
+                    turn(n, t, c)
+            fused_grandparents(t, 0, 2)
+        parents(2)
+        vector_grandparents(2, 1)
+        add_parents(2)
+        fused_grandparents(2, 0, 2)
+        for c in TURNED:
+            turn(1, 2, c)
+        turn(2, 2, 2)
+        parents(last)
+        scalar_grandparents(2, 3)
+        add_parents(last)
+        scalar_grandparents(last, 2)
+        for c in TURNED:
+            turn(1, last, c)
+        turn(2, 2, 3)
+        turn(2, last, 2)
+        scalar_grandparents(last, 3)
+        turn(2, last, 3)
+        rectify_turned(0, 2)
+        rectify_turned(0, 3)
         fused_grandparents(last, 0, 1)
         fused_grandparents(last, 1, 1)
-
         rectify("vector", 0)
-        rectify("scalar", 1)
-        late_grandparents(last)
-        subtract_sums(0, 2, 2)
+        rectify("vector", 1)
+        for c in TURNED:
+            rectify_turned(1, c)
         quantise_z(0)
+        quantise_z(1, keep.tile([P, PIECE], U8, name="zs1", tag="turned1_2", align_bytes=64)[:])
+        for c in TURNED:
+            join_pairs("scalar", c)
+        layer2(0, 0, PACK, 4, "scalar", 2)
         for h in range(2):
-            layer2(0, 2 * h, 2, h)
-            values_out("scalar", 0, 2 * h, 2)
-            store_early(0, 2 * h, 2)
-        subtract_sums(1, 2, 2)
-        quantise_z(1)
-        for h in range(2):
-            layer2(1, 2 * h, 2, 2 + h)
-            values_out("scalar", 1, 2 * h, 2)
-        store_early(1, 0, PACK)
-        round_values("scalar", 0)
-
-        subtract_sums(2, 2, 2)
-        subtract_sums(last, 2, 1)
-        subtract_sums(last, 3, 1)
-        rectify("vector", 2)
-        rectify("vector", 3)
+            store_values(nc.sync, 0, 2 * h, 2)
         quantise_z(2)
         quantise_z(3)
-        layer2(2, 0, 2, 4)
-        layer2(3, 0, 1, 5)
-        layer2(3, 1, 1, 6)
-        layer2(2, 2, 2, 3)
-        layer2(3, 2, 2, 7)
-        round_values("vector", 1)
-        values_out("scalar", 2, 0, 2)
-        for t in range(2):
-            values_out("scalar", 3, t, 1)
-            store_late(nc.sync, t, 1)
-        quantise_values(1)
-        values_out("vector", 2, 2, 2)
-        values_out("scalar", 3, 2, 2)
-        store_late(nc.scalar, 2, 2)
+        layer2(1, 0, 2, 3, "scalar")
+        layer2(1, 2, 2, 7, "vector")
+        store_values(nc.sync, 1, 0, PACK)
+        round_values("vector", 0)
+        layer2(2, 0, 2, 0, "scalar")
+        layer2(2, 2, 2, 2, "vector")
+        layer2(3, 0, 2, 5, "scalar")
+        store_late(nc.sync, 0, 2)
+        layer2(3, 2, 1, 6, "vector")
+        layer2(3, 3, 1, 1, "scalar")
+        store_late(nc.sync, 2, 2)
         quantise_values(0)
         round_values("vector", 2)
+        round_values("scalar", 1)
         round_values("vector", 3)
         quantise_values(2)
         quantise_values(3)
-
-        nc.sync.dma_start(out_1[0].rearrange("p n t -> p (n t)").bitcast(I32), out_words[:].bitcast(I32))
+        quantise_values(1)
+        nc.sync.dma_start(words_rows, out_words[:].bitcast(I32))
         for r in range(4):
             nc.scalar.dma_start(out_2[0][r:16:4, :].bitcast(I32), out_scales[r:P:32, :].bitcast(I32))

@@ -315,9 +315,8 @@ def tile_picked_ptrjump_relu_po_kernel(
         quantise_z(1, keep.tile([P, PIECE], U8, name="zs1", tag="turned1_2", align_bytes=64)[:])
         for c in TURNED:
             join_pairs("scalar", c)
-        layer2(0, 0, PACK, 4, "scalar", 2)
-        for h in range(2):
-            store_values(nc.sync, 0, 2 * h, 2)
+        layer2(0, 0, PACK, 4, "scalar")
+        store_values(nc.sync, 0, 0, PACK)
         quantise_z(2)
         quantise_z(3)
         layer2(1, 0, 2, 3, "scalar")
@@ -327,10 +326,9 @@ def tile_picked_ptrjump_relu_po_kernel(
         layer2(2, 0, 2, 0, "scalar")
         layer2(2, 2, 2, 2, "vector")
         layer2(3, 0, 2, 5, "scalar")
-        store_late(nc.sync, 0, 2)
         layer2(3, 2, 1, 6, "vector")
         layer2(3, 3, 1, 1, "scalar")
-        store_late(nc.sync, 2, 2)
+        store_late(nc.sync, 0, PACK)
         quantise_values(0)
         round_values("vector", 2)
         round_values("scalar", 1)

from contextlib import ExitStack

import concourse.mybir as mybir
from concourse.masks import make_identity

K, T, S, H, N = 512, 2048, 512, 512, 512
FLOPS = 2 * K * H * S + 2 * H * N * S

F32 = mybir.dt.float32
BF16 = mybir.dt.bfloat16
I32 = mybir.dt.int32
U32 = mybir.dt.uint32
U16 = mybir.dt.uint16
U8 = mybir.dt.uint8
FP8X4 = mybir.dt.float8_e4m3fn_x4
ALU = mybir.AluOpType
ACT = mybir.ActivationFunctionType

P = 128
PACK = 4
HALF = S // 2
PIECE = 128
PIECES = S // PIECE
BANKS = 8
FIRST_PAIR_SPLIT = 96
SECOND_PAIR_SPLIT = 56
ROWS_AT = slice(16, 32)
CLEARED = ((0, 16), (32, 64), (64, P))


def tile_picked_ptrjump_relu_po_kernel(
    tc, x_words, x_scales, w1, w2_words, w2_scales, offs, par, out_0, out_1, out_2
):
    nc = tc.nc
    with ExitStack() as ctx:
        lists = ctx.enter_context(tc.tile_pool(name="lists", bufs=1))
        keep = ctx.enter_context(tc.tile_pool(name="keep", bufs=1))
        psum = ctx.enter_context(tc.psum_pool(name="psum", bufs=1))

        offs_t = lists.tile([P, S // 16], U16, name="offs_t")
        par_t = lists.tile([P, S // 16], U16, name="par_t")
        w1_raw = keep.tile([P, PACK, H], F32, name="w1_raw", align_bytes=64)
        x_table = keep.tile([P, T], U32, name="x_table", align_bytes=64)
        xs_table = keep.tile([P, T], U8, name="xs_table", align_bytes=64)
        w2s_raw = keep.tile([P, N], U8, name="w2s_raw", align_bytes=64)

        xs = keep.tile([P, S], U8, name="xs", align_bytes=64)
        w2_s = keep.tile([P, N], U8, name="w2_s", align_bytes=64)
        nc.sync.dma_start(xs_table[ROWS_AT, :].bitcast(I32), x_scales[0].bitcast(I32))
        for lo, hi in CLEARED:
            nc.vector.memset(xs_table[lo:hi, :].bitcast(I32), 0)
        nc.gpsimd.memset(xs[:].bitcast(I32), 0)
        for lo, hi in CLEARED:
            nc.gpsimd.memset(w2s_raw[lo:hi, :].bitcast(I32), 0)
        nc.gpsimd.memset(w2_s[:].bitcast(I32), 0)
        identity = keep.tile([P, P], F32, name="identity", align_bytes=64)
        make_identity(nc, identity[:])
        nc.sync.dma_start(offs_t[:], offs)
        nc.sync.dma_start(x_table[:].bitcast(I32), x_words[0].rearrange("p n t -> p (n t)").bitcast(I32))
        nc.sync.dma_start(w2s_raw[ROWS_AT, :].bitcast(I32), w2_scales[0].bitcast(I32))
        nc.sync.dma_start(w1_raw[:], w1.rearrange("(p j) c -> p j c", j=PACK))
        nc.sync.dma_start(par_t[:], par)

        def move_rows(plane, spread):
            for r in range(4):
                nc.sync.dma_start(plane[r:P:32, :].bitcast(I32), spread[16 + r : 32 : 4, :].bitcast(I32))

        def dealt(ap):
            return ap.rearrange("p (t m) -> p m t", t=PACK)

        def undealt(ap):
            return ap.rearrange("p (m t) -> p m t", t=PACK)

        xs_spread = keep.tile([P, S], U8, name="xs_spread", align_bytes=64)
        nc.vector.tensor_copy(xs_spread[:], xs_table[:].indirect(offs_t[:]))
        move_rows(xs, xs_spread)
        w2_raw = keep.tile([P, N], I32, name="w2_raw", tag="xs_table", align_bytes=64)
        nc.sync.dma_start(w2_raw[:], w2_words[0].rearrange("p n t -> p (n t)").bitcast(I32))

        xw = keep.tile([P, S], U32, name="xw", align_bytes=64)
        nc.vector.tensor_copy(xw[:], x_table[:].indirect(offs_t[:]))

        w2s_spread = keep.tile([P, N], U8, name="w2s_spread", align_bytes=64)
        nc.vector.tensor_copy(dealt(w2s_spread[:]), undealt(w2s_raw[:]))
        move_rows(w2_s, w2s_spread)

        w1_src = w1_raw[:].rearrange("p j (m t) -> p m j t", t=PACK)
        w1_q = keep.tile([P, H], U32, name="w1_q", align_bytes=64)
        w1_s = keep.tile([P, H], U8, name="w1_s", align_bytes=64)
        w1_b = [keep.tile([P, 2 * H], BF16, name="w1_b%d" % u, align_bytes=64) for u in range(2)]
        w1_dst = [w1_b[u][:].rearrange("p (t m j) -> p m j t", t=2, j=PACK) for u in range(2)]

        def round_w1(engine, pair, lo, hi):
            src = w1_src[:, lo:hi, :, 2 * pair : 2 * pair + 2]
            if engine == "scalar":
                nc.scalar.activation(w1_dst[pair][:, lo:hi], src, ACT.Copy)
            else:
                nc.vector.tensor_copy(w1_dst[pair][:, lo:hi], src)

        def quantise_w1(lo, hi):
            pair = lo // (2 * P)
            src = w1_b[pair][:, PACK * (lo - 2 * P * pair) : PACK * (hi - 2 * P * pair)]
            nc.vector.quantize_mx(out=w1_q[:, lo:hi].bitcast(FP8X4), scales=w1_s[:, lo:hi], in_=src)

        round_w1("scalar", 0, FIRST_PAIR_SPLIT, P)
        round_w1("vector", 0, 0, P // 2)
        round_w1("vector", 0, P // 2, FIRST_PAIR_SPLIT)
        round_w1("scalar", 1, SECOND_PAIR_SPLIT, P)
        quantise_w1(0, P // 2)
        quantise_w1(P // 2, P)
        round_w1("vector", 1, 0, SECOND_PAIR_SPLIT)
        quantise_w1(P, 2 * P)

        w2_q = keep.tile([P, N], I32, name="w2_q", tag="x_table", align_bytes=64)
        nc.vector.tensor_copy(dealt(w2_q[:]), undealt(w2_raw[:]))

        def cols_of(c, count=1):
            return slice(c * PIECE, (c + count) * PIECE)

        def list_of(c, count=1):
            return par_t[:, c * PIECE // 16 : (c + count) * PIECE // 16]

        def copy_out(engine, dst, bank):
            if engine == "scalar":
                nc.scalar.copy(dst, bank)
            else:
                nc.vector.tensor_copy(dst, bank)

        y_win = [keep.tile([P, 2 * S], F32, name="y_win%d" % t, align_bytes=64) for t in range(PACK)]
        p_win = [keep.tile([P, S], F32, name="p_win%d" % t, align_bytes=64) for t in range(PACK)]

        def layer1(engine, t, cols, number):
            bank = psum.tile([P, cols.stop - cols.start], F32, name="y%d_%d" % (t, cols.start), tag="bank%d" % number)
            rows = slice(t * P, (t + 1) * P)
            nc.tensor.matmul_mx(
                out=bank[:],
                lhsT=w1_q[:, rows].bitcast(FP8X4),
                lhsT_scale=w1_s[:, rows],
                rhs=xw[:, cols].bitcast(FP8X4),
                rhs_scale=xs[:, cols],
                start=True,
                stop=True,
            )
            copy_out(engine, y_win[t][:, cols], bank[:])

        for c in range(PIECES):
            layer1("scalar", 0, cols_of(c), c)
        quantise_w1(2 * P, PACK * P)
        for t in range(1, PACK):
            for h in range(2):
                engine = "scalar" if (t, h) == (1, 0) else "vector"
                layer1(engine, t, cols_of(2 * h, 2), (PIECES + 2 * (t - 1) + h) % BANKS)

        TURNED = (2, 3)
        last = PACK - 1

        def parents(t):
            nc.scalar.activation(p_win[t][:], y_win[t][:].indirect(par_t[:]), ACT.Copy)

        sums = [
            keep.tile([P, HALF], F32, name="sum%d" % t, tag="w1_q" if t == 0 else "sum%d" % t, align_bytes=64)
            for t in range(PACK)
        ]

        def add_parents(t):
            nc.vector.tensor_tensor(sums[t][:], y_win[t][:, :HALF], p_win[t][:, :HALF], ALU.add)

        minus_room = keep.tile([P, PACK * HALF], F32, name="minus_room", align_bytes=64)
        minus_rows = minus_room[:].rearrange("p (t n) -> p t n", t=PACK)
        minus_z = [minus_rows[:, :, cols_of(c)] for c in range(2)]

        def fused_grandparents(t, c, count):
            window = p_win[t][:].indirect(list_of(c, count))
            nc.vector.tensor_tensor(minus_rows[:, t, cols_of(c, count)], window, sums[t][:, cols_of(c, count)], ALU.subtract)

        minus_q = [keep.tile([P, HALF], F32, name="minus_q%d" % t, align_bytes=64) for t in range(PACK)]

        def vector_grandparents(t, count):
            window = p_win[t][:].indirect(list_of(TURNED[0], count))
            nc.vector.tensor_scalar(minus_q[t][:, cols_of(0, count)], window, -1.0, 0.0, ALU.mult, ALU.add)

        def scalar_grandparents(t, c):
            window = p_win[t][:].indirect(list_of(c))
            nc.scalar.activation(minus_q[t][:, cols_of(c - TURNED[0])], window, ACT.Copy, scale=-1.0)

        low = psum.tile([P, 2, 2, P], F32, name="low", tag="bank1")
        high = {c: psum.tile([P, 2, P], F32, name="high%d" % c, tag="bank%d" % (1 + c)) for c in TURNED}
        pairs = {c: psum.tile([P, 2, PIECE], F32, name="pairs%d" % c, tag="bank%d" % (3 + c)) for c in TURNED}

        def turn(n, t, c):
            out = low[:, c - TURNED[0], t, :] if t < 2 else high[c][:, t - 2, :]
            source = (y_win[t][:, cols_of(c)], p_win[t][:, cols_of(c)], minus_q[t][:, cols_of(c - TURNED[0])])[n]
            opens = n == 0 and (t == 2 or (t, c) == (0, TURNED[0]))
            closes = n == 2 and (t == last or (t, c) == (1, TURNED[1]))
            nc.tensor.matmul(out, source, identity[:], start=opens, stop=closes, is_transpose=True)

        seen = {}

        def rectify_turned(u, c):
            src = low[:, c - TURNED[0]] if u == 0 else high[c][:]
            turned = keep.tile([P, 2 * P], BF16, name="turned%d_%d" % (u, c), align_bytes=64)
            nc.scalar.activation(
                turned[:].rearrange("p (r e) -> p r e", e=2), src.rearrange("p e r -> p r e"), ACT.Relu
            )
            seen[u, c] = turned
            nc.tensor.transpose(pairs[c][:, u, :], turned[:].bitcast(F32), identity[:])

        out_words = keep.tile([P, S], U32, name="out_words", align_bytes=64)
        out_scales = keep.tile([P, S], U8, name="out_scales", align_bytes=64)
        out_rows = out_0.rearrange("(p t) c -> p t c", t=PACK)
        words_rows = out_1[0].rearrange("p n t -> p (n t)").bitcast(I32)
        z_rounded = [keep.tile([P, PACK * PIECE], BF16, name="zb%d" % c, align_bytes=64) for c in range(PIECES)]
        late_values = keep.tile([P, PACK, HALF], F32, name="late_values", align_bytes=64)
        values = [keep.tile([P, PACK, PIECE], F32, name="values%d" % c, align_bytes=64)[:] for c in range(2)]
        values = values + [late_values[:, :, cols_of(c)] for c in range(2)]
        z_packed = {}
        values_rounded = {}

        def woven(ap):
            return ap.rearrange("p (c i t) -> p c t i", i=4, t=PACK)

        def row_tiles(ap):
            return ap.rearrange("p t (c i) -> p c t i", i=4)

        def join_pairs(engine, c):
            dst = z_rounded[c][:].bitcast(F32).rearrange("p (n u) -> p n u", u=2)
            copy_out(engine, dst, pairs[c][:].rearrange("p u n -> p n u"))

        def rectify(engine, c):
            if engine == "scalar":
                nc.scalar.activation(woven(z_rounded[c][:]), row_tiles(minus_z[c]), ACT.Relu, scale=-1.0)
            else:
                nc.vector.tensor_scalar(woven(z_rounded[c][:]), row_tiles(minus_z[c]), -1.0, 0.0, ALU.mult, ALU.max)

        def quantise_z(c, scales=None):
            codes = keep.tile([P, PIECE], U32, name="zq%d" % c, align_bytes=64)
            if scales is None:
                scales = keep.tile([P, PIECE], U8, name="zs%d" % c, align_bytes=64)[:]
            nc.vector.quantize_mx(out=codes[:].bitcast(FP8X4), scales=scales, in_=z_rounded[c][:])
            z_packed[c] = (codes, scales)

        def layer2(c, first, count, number, engine, step=PACK):
            codes, scales = z_packed[c]
            bank = psum.tile([P, count, PIECE], F32, name="acc%d_%d" % (c, first), tag="bank%d" % number)
            for u in range(count):
                rows = slice((first + u) * P, (first + u + 1) * P)
                nc.tensor.matmul_mx(
                    out=bank[:, u, :],
                    lhsT=w2_q[:, rows].bitcast(FP8X4),
                    lhsT_scale=w2_s[:, rows],
                    rhs=codes[:].bitcast(FP8X4),
                    rhs_scale=scales,
                    start=True,
                    stop=True,
                )
            for u in range(0, count, step):
                width = min(step, count)
                copy_out(engine, values[c][:, first + u : first + u + width, :], bank[:, u : u + width, :])

        def store_values(queue, c, first, count):
            queue.dma_start(out_rows[:, first : first + count, cols_of(c)], values[c][:, first : first + count, :])

        def store_late(queue, first, count):
            queue.dma_start(out_rows[:, first : first + count, HALF:], late_values[:, first : first + count, :])

        def round_values(engine, c):
            tag = "zs3" if c == 1 else "ob%d" % c
            values_rounded[c] = keep.tile([P, PACK * PIECE], BF16, name="ob%d" % c, tag=tag, align_bytes=64)
            if engine == "scalar":
                nc.scalar.activation(woven(values_rounded[c][:]), row_tiles(values[c]), ACT.Copy)
            else:
                nc.vector.tensor_copy(woven(values_rounded[c][:]), row_tiles(values[c]))

        def quantise_values(c):
            cols = cols_of(c)
            nc.vector.quantize_mx(out=out_words[:, cols].bitcast(FP8X4), scales=out_scales[:, cols], in_=values_rounded[c][:])

        for t in range(PACK):
            for c in TURNED:
                turn(0, t, c)
        for t in range(2):
            parents(t)
            add_parents(t)
            vector_grandparents(t, 2)
            for n in (1, 2):
                for c in TURNED:
                    turn(n, t, c)
            fused_grandparents(t, 0, 2)
        parents(2)
        vector_grandparents(2, 1)
        add_parents(2)
        fused_grandparents(2, 0, 2)
        for c in TURNED:
            turn(1, 2, c)
        turn(2, 2, 2)
        parents(last)
        scalar_grandparents(2, 3)
        add_parents(last)
        scalar_grandparents(last, 2)
        for c in TURNED:
            turn(1, last, c)
        turn(2, 2, 3)
        turn(2, last, 2)
        scalar_grandparents(last, 3)
        turn(2, last, 3)
        rectify_turned(0, 2)
        rectify_turned(0, 3)
        fused_grandparents(last, 0, 1)
        fused_grandparents(last, 1, 1)
        rectify("vector", 0)
        rectify("vector", 1)
        for c in TURNED:
            rectify_turned(1, c)
        quantise_z(0)
        quantise_z(1, keep.tile([P, PIECE], U8, name="zs1", tag="turned1_2", align_bytes=64)[:])
        for c in TURNED:
            join_pairs("scalar", c)
        layer2(0, 0, PACK, 4, "scalar")
        store_values(nc.sync, 0, 0, PACK)
        quantise_z(2)
        quantise_z(3)
        layer2(1, 0, 2, 3, "scalar")
        layer2(1, 2, 2, 7, "vector")
        store_values(nc.sync, 1, 0, PACK)
        round_values("vector", 0)
        layer2(2, 0, 2, 0, "scalar")
        layer2(2, 2, 2, 2, "vector")
        layer2(3, 0, 2, 5, "scalar")
        layer2(3, 2, 1, 6, "vector")
        layer2(3, 3, 1, 1, "scalar")
        store_late(nc.sync, 0, PACK)
        quantise_values(0)
        round_values("vector", 2)
        round_values("scalar", 1)
        round_values("vector", 3)
        quantise_values(2)
        quantise_values(3)
        quantise_values(1)
        nc.sync.dma_start(words_rows, out_words[:].bitcast(I32))
        for r in range(4):
            nc.scalar.dma_start(out_2[0][r:16:4, :].bitcast(I32), out_scales[r:P:32, :].bitcast(I32))
